import numpy as np
import ml_dtypes


def mxq(x, axis, fmt="e4m3"):
    dtype, down = {"e4m3": (ml_dtypes.float8_e4m3fn, 7), "e5m2": (ml_dtypes.float8_e5m2, 14)}[fmt]
    v = np.moveaxis(np.asarray(x, np.float32).astype(ml_dtypes.bfloat16).astype(np.float64), axis, -1)
    blocks = v.reshape(v.shape[:-1] + (-1, 32))
    amax = np.abs(blocks).max(-1, keepdims=True)
    byte = np.maximum(np.where(amax > 0, np.frexp(amax)[1] - 1 + 127, 0) - down, 1)
    scale = np.exp2(byte - 127.0)
    codes = (blocks / scale).astype(np.float32).astype(dtype).astype(np.float64)
    return np.moveaxis((codes * scale).reshape(v.shape), -1, axis)


WIDE = False


def mx_kscale(k):
    if not WIDE:
        return np.ones(k)
    levels = np.array([10, -10, 5, -5, 0])
    if k % 512:
        return np.exp2(np.random.permutation(np.resize(levels, k // 32))).repeat(32)
    a = np.empty((k // 512, 16))
    for p in range(k // 512):
        a[p, :8] = np.random.permutation(np.resize(levels, 8))
        for g in range(8):
            far = levels[np.abs(levels - a[p, g]) >= 10]
            a[p, g + 8] = far[np.random.randint(len(far))]
    return np.exp2(a.ravel()).repeat(32)


def f64(x):
    return np.asarray(x).astype(np.float64)


def striped(idx):
    return np.tile(np.asarray(idx).reshape(-1, 16).T, (8, 1)).astype(np.uint16)


def unstriped(offs):
    return offs[:16].T.reshape(-1).astype(np.int64)


B, N, T, D, DV, NQ = 1, 512, 1024, 512, 256, 256


def setup_inputs():
    n = np.random.standard_normal
    idx = np.sort(np.random.permutation(T)[:B * N].reshape(B, N), axis=1).reshape(-1)
    s = mx_kscale(D)[:, None]
    u = np.ones(T)
    u[idx] = mx_kscale(B * N)
    r = np.random.uniform(0.5, 2.0, T)
    rk = np.random.uniform(0.5, 2.0, T)
    k = n((D, T)) / s / rk
    v = n((DV, T)) / (u * r)
    return {
        "qT": (n((B, D, NQ)) * s * (0.60 / np.sqrt(D))).astype(np.float32),
        "kT": k.astype(np.float32),
        "vT": v.astype(np.float32),
        "ks": np.tile(rk, (128, 1)).astype(np.float32),
        "vs": np.tile(u * r, (128, 1)).astype(np.float32),
        "kb": np.tile(n(T), (128, 1)).astype(np.float32),
        "offs": striped(idx),
    }


def reference(qT, kT, vT, ks, vs, kb, offs):
    idx = unstriped(offs)
    k = f64(kT)
    v = f64(vT)
    pick = lambda x: x[:, idx].reshape(x.shape[0], B, N).transpose(1, 0, 2)
    q = f64(qT)
    score = mxq(q, 1, "e4m3").transpose(0, 2, 1) @ mxq(pick(k), 1, "e4m3")
    score = score * pick(f64(ks))[:, :1, :]
    score = score + pick(f64(kb))[:, :1, :]
    m = score.max(-1, keepdims=True)
    p = np.exp(score - m)
    total = p.sum(-1, keepdims=True)
    w = p * pick(f64(vs))[:, :1, :]
    y = mxq(w, 2, "e4m3") @ mxq(pick(v).transpose(0, 2, 1), 1, "e4m3")
    y = y / total
    return y

@@ -1,0 +1,217 @@
+from contextlib import ExitStack
+
+import concourse.mybir as mybir
+from concourse.masks import make_identity
+
+P = 128
+D, T, N, NQ, DV = 512, 1024, 512, 256, 256
+F32 = mybir.dt.float32
+BF16 = mybir.dt.bfloat16
+U32 = mybir.dt.uint32
+U16 = mybir.dt.uint16
+U8 = mybir.dt.uint8
+FP8X4 = mybir.dt.float8_e4m3fn_x4
+ACT = mybir.ActivationFunctionType
+ALU = mybir.AluOpType
+AX = mybir.AxisListType
+
+FLOPS = 2 * NQ * N * (D + DV)
+BYTES = 4 * (D * NQ + (D + DV) * N + 3 * N + NQ * DV) + 2 * N
+
+
+def tile_attend_x_ks_bias_srt_kernel(tc, qT, kT, vT, ks, vs, kb, offs, out):
+    nc = tc.nc
+    with ExitStack() as ctx:
+        keep = ctx.enter_context(tc.tile_pool(name="keep", bufs=1))
+        psum = ctx.enter_context(tc.psum_pool(name="psum", bufs=2))
+
+        offsets = keep.tile([P, N // 16], U16, name="offsets")
+        ks_row = keep.tile([P, T], F32, name="ks_row")
+        kb_row = keep.tile([P, T], F32, name="kb_row")
+        vs_row = keep.tile([P, T], F32, name="vs_row")
+        warm = keep.tile([P, 1], F32, name="warm")
+        ident = keep.tile([P, P], F32, name="ident")
+
+        nc.sync.dma_start(offsets[:], offs)
+        nc.vector.memset(warm[:], 0.0)
+        nc.scalar.activation(out=warm[:], in_=warm[:], func=ACT.Exp)
+        for row, cut in ((ks_row, 808), (kb_row, 512), (vs_row, 384)):
+            nc.gpsimd.memset(row[:, :cut], 0.0)
+            nc.vector.memset(row[:, cut:], 0.0)
+        make_identity(nc, ident[:])
+
+        k_view = kT.rearrange("(p j) n -> p j n", j=4)
+        k_pool = [keep.tile([P, T * 2], BF16, name=f"k_pool{u}", align_bytes=64) for u in range(2)]
+
+        def load_pair(j, lo, hi, name):
+            t = keep.tile([P, 2, hi - lo], F32, name=name, tag=name)
+            nc.sync.dma_start(t[:], k_view[:, j : j + 2, lo:hi])
+            return t
+
+        def cast_pair(engine_copy, pool, raw, lo, hi, base):
+            engine_copy(
+                pool[:, 2 * lo : 2 * hi].rearrange("p (n h) -> p n h", h=2),
+                raw[:, :, lo - base : hi - base].rearrange("p h n -> p n h"),
+            )
+
+        def scalar_cast(o, i):
+            nc.scalar.activation(out=o, in_=i, func=ACT.Copy)
+
+        def gather_table(row, g):
+            nc.vector.tensor_copy(g, row[:].indirect(offsets[:]))
+
+        def turn_table(g, step, name, tag):
+            bank = psum.tile([P, 4, P], F32, name=name + "_t", tag=tag)
+            for c in range(4):
+                src = g[:, c * P : (c + 1) * P] if step == 1 else g[:, c : N : 4]
+                nc.tensor.transpose(bank[:, c, :], src, ident[:])
+            return bank
+
+        def column(bank, name, tag):
+            col = keep.tile([P, 4], F32, name=name + "_c", tag=tag)
+            nc.scalar.activation(out=col[:], in_=bank[:, :, 0], func=ACT.Copy)
+            return col
+
+        k0a = load_pair(0, 0, 512, "k0a")
+        nc.sync.dma_start(ks_row[0:1, :], ks[0:1, :])
+        k0b = load_pair(0, 512, T, "k0b")
+        nc.sync.dma_start(kb_row[0:1, :], kb[0:1, :])
+        k1a = load_pair(2, 0, 512, "k1a")
+        k1b = load_pair(2, 512, T, "k1b")
+        q_raw = keep.tile([P, 4, NQ], F32, name="q_raw", tag="q_raw")
+        nc.sync.dma_start(q_raw[:], qT[0].rearrange("(p j) n -> p j n", j=4))
+        nc.sync.dma_start(vs_row[0:1, :], vs[0:1, :])
+        v_raw = []
+        for e in range(2):
+            t = keep.tile([P, T], F32, name=f"v_raw{e}")
+            nc.sync.dma_start(t[:], vT[e * P : (e + 1) * P, :])
+            v_raw.append(t)
+
+        tab_g = keep.tile([P, 2, N], F32, name="tab_g", align_bytes=64)
+        gather_table(ks_row, tab_g[:, 0, :])
+        ks_bank = turn_table(tab_g[:, 0, :], 1, "ks", "x")
+        gather_table(kb_row, tab_g[:, 1, :])
+        kb_bank = turn_table(tab_g[:, 1, :], 1, "kb", "x")
+
+        grp = keep.tile([P, (NQ + N) * 4], BF16, name="grp", tag="grp", align_bytes=64)
+        codes = keep.tile([P, NQ + N], U32, name="codes", align_bytes=64)
+        scales = keep.tile([P, NQ + N], U8, name="scales", align_bytes=64)
+        k_words = grp[:, NQ * 4 :].bitcast(U32).rearrange("p (i u) -> p i u", u=2)
+
+        cast_pair(scalar_cast, k_pool[0], k0a, 0, 512, 0)
+        cast_pair(scalar_cast, k_pool[0], k0b, 512, T, 512)
+        nc.vector.tensor_copy(k_words[:, :, 0], k_pool[0][:].bitcast(U32).indirect(offsets[:]))
+        cast_pair(scalar_cast, k_pool[1], k1a, 0, 512, 0)
+        cast_pair(scalar_cast, k_pool[1], k1b, 512, 704, 512)
+        cast_pair(nc.vector.tensor_copy, k_pool[1], k1b, 704, T, 512)
+        for h in range(2):
+            nc.vector.tensor_copy(
+                k_words[:, h * 256 : (h + 1) * 256, 1],
+                k_pool[1][:].bitcast(U32).indirect(offsets[:, h * 16 : (h + 1) * 16]),
+            )
+        scalar_cast(grp[:, : NQ * 4].rearrange("p (n j) -> p n j", j=4), q_raw[:].rearrange("p j n -> p n j"))
+        ks_col = column(ks_bank, "ks", "k1a")
+        kb_col = column(kb_bank, "kb", "k1b")
+        for lo, hi in ((NQ, NQ + 256), (NQ + 256, NQ + N), (0, NQ)):
+            nc.vector.quantize_mx(
+                out=codes[:, lo:hi].bitcast(FP8X4), scales=scales[:, lo:hi], in_=grp[:, lo * 4 : hi * 4]
+            )
+
+        s_t = keep.tile([P, 4, NQ], F32, name="s_t")
+        for c in range(4):
+            bank = psum.tile([P, NQ], F32, name="qk", tag="x" if c < 2 else "w")
+            sl = slice(NQ + c * P, NQ + (c + 1) * P)
+            nc.tensor.matmul_mx(
+                out=bank[:],
+                lhsT=codes[:, sl].bitcast(FP8X4),
+                lhsT_scale=scales[:, sl],
+                rhs=codes[:, :NQ].bitcast(FP8X4),
+                rhs_scale=scales[:, :NQ],
+                start=True,
+                stop=True,
+            )
+            nc.scalar.activation(
+                out=s_t[:, c, :], in_=bank[:], func=ACT.Identity,
+                scale=ks_col[:, c : c + 1], bias=kb_col[:, c : c + 1],
+            )
+
+        g_all = keep.tile([P, 3, N], F32, name="g_all", tag="grp", align_bytes=64)
+        gather_table(vs_row, g_all[:, 0, :])
+        for e in range(2):
+            gather_table(v_raw[e], g_all[:, 1 + e, :])
+        vs_bank = turn_table(g_all[:, 0, :], 4, "vs", "z")
+        vs_col = column(vs_bank, "vs", "k1a")
+
+        s_banks = []
+        for b in range(2):
+            bank = psum.tile([P, N], F32, name="s_b", tag="y")
+            for c in range(4):
+                nc.tensor.transpose(bank[:, c * P : (c + 1) * P], s_t[:, c, b * P : (b + 1) * P], ident[:])
+            s_banks.append(bank)
+        v_banks = [turn_table(g_all[:, 1 + e, :], 4, f"v{e}", "z") for e in range(2)]
+
+        neg_ms = []
+        for b in range(2):
+            neg_m = keep.tile([P, 1], F32, name=f"neg_m{b}", tag=f"neg_m{b}", align_bytes=64)
+            nc.vector.tensor_reduce(out=neg_m[:], in_=s_banks[b][:], axis=AX.X, op=ALU.max, negate=True)
+            neg_ms.append(neg_m)
+        v_codes = keep.tile([P, DV], U32, name="v_codes", align_bytes=64)
+        v_scale = keep.tile([P, DV], U8, name="v_scale", align_bytes=64)
+
+        def value_group(engine_copy, bank, e, tag):
+            v_grp = keep.tile([P, P * 4], BF16, name=f"v_grp{e}", tag=tag, align_bytes=64)
+            engine_copy(v_grp[:].rearrange("p (e t) -> p e t", t=4), bank[:].rearrange("p t e -> p e t"))
+            return v_grp
+
+        def quantize_values(v_grp, e):
+            cols = slice(e * P, (e + 1) * P)
+            nc.vector.quantize_mx(out=v_codes[:, cols].bitcast(FP8X4), scales=v_scale[:, cols], in_=v_grp[:])
+
+        quantize_values(value_group(nc.vector.tensor_copy, v_banks[0], 0, "v_grp0"), 0)
+        p_tiles = []
+        l_tiles = []
+        for b in range(2):
+            p = keep.tile([P, 4, P], F32, name=f"p{b}")
+            l = keep.tile([P, 1], F32, name=f"l{b}")
+            nc.scalar.activation(
+                out=p[:],
+                in_=s_banks[b][:].rearrange("p (s t) -> p t s", t=4),
+                func=ACT.Exp,
+                bias=neg_ms[b][:],
+                accum_out=l[:],
+            )
+            p_tiles.append(p)
+            l_tiles.append(l)
+        v_grp1 = value_group(scalar_cast, v_banks[1], 1, "neg_m1")
+
+        for b in range(2):
+            bank = psum.tile([P, 4, P], F32, name="p_t", tag="x")
+            for t in range(4):
+                nc.tensor.transpose(bank[:, t, :], p_tiles[b][:, t, :], ident[:])
+            w_grp = keep.tile([P, P * 4], BF16, name=f"w_grp{b}", align_bytes=64)
+            nc.vector.tensor_tensor(
+                out=w_grp[:].rearrange("p (q t) -> p q t", t=4),
+                in0=bank[:].rearrange("p t q -> p q t"),
+                in1=vs_col[:].unsqueeze(1).to_broadcast([P, P, 4]),
+                op=ALU.mult,
+            )
+            w_codes = keep.tile([P, P], U32, name=f"w_codes{b}", align_bytes=64)
+            w_scale = keep.tile([P, P], U8, name=f"w_scale{b}", align_bytes=64)
+            nc.vector.quantize_mx(out=w_codes[:].bitcast(FP8X4), scales=w_scale[:], in_=w_grp[:])
+            if b == 0:
+                quantize_values(v_grp1, 1)
+            rl = keep.tile([P, 1], F32, name=f"rl{b}")
+            nc.vector.reciprocal(rl[:], l_tiles[b][:])
+            acc = psum.tile([P, DV], F32, name="acc", tag="w")
+            nc.tensor.matmul_mx(
+                out=acc[:],
+                lhsT=w_codes[:].bitcast(FP8X4),
+                lhsT_scale=w_scale[:],
+                rhs=v_codes[:].bitcast(FP8X4),
+                rhs_scale=v_scale[:],
+                start=True,
+                stop=True,
+            )
+            y = keep.tile([P, DV], F32, name=f"y{b}")
+            nc.scalar.activation(out=y[:], in_=acc[:], func=ACT.Copy, scale=rl[:])
+            nc.sync.dma_start(out[0, b * P : (b + 1) * P, :], y[:])

@@ -23,7 +23,7 @@ def tile_attend_x_ks_bias_srt_kernel(tc, qT, kT, vT, ks, vs, kb, offs, out):
     nc = tc.nc
     with ExitStack() as ctx:
         keep = ctx.enter_context(tc.tile_pool(name="keep", bufs=1))
-        psum = ctx.enter_context(tc.psum_pool(name="psum", bufs=2))
+        psum = ctx.enter_context(tc.psum_pool(name="psum", bufs=1))
 
         offsets = keep.tile([P, N // 16], U16, name="offsets")
         ks_row = keep.tile([P, T], F32, name="ks_row")
@@ -33,34 +33,39 @@ def tile_attend_x_ks_bias_srt_kernel(tc, qT, kT, vT, ks, vs, kb, offs, out):
         ident = keep.tile([P, P], F32, name="ident")
 
         nc.sync.dma_start(offsets[:], offs)
+        nc.sync.dma_start(ks_row[0:32, :], ks[0:32, :])
+        nc.gpsimd.memset(kb_row[:, :512], 0.0)
+        nc.vector.memset(kb_row[:, 512:], 0.0)
         nc.vector.memset(warm[:], 0.0)
         nc.scalar.activation(out=warm[:], in_=warm[:], func=ACT.Exp)
-        for row, cut in ((ks_row, 808), (kb_row, 512), (vs_row, 384)):
-            nc.gpsimd.memset(row[:, :cut], 0.0)
-            nc.vector.memset(row[:, cut:], 0.0)
+        nc.gpsimd.memset(vs_row[:, :512], 0.0)
+        nc.vector.memset(vs_row[:, 512:], 0.0)
+        nc.gpsimd.memset(ks_row[32:64, :], 0.0)
+        nc.vector.memset(ks_row[64:128, :], 0.0)
         make_identity(nc, ident[:])
 
         k_view = kT.rearrange("(p j) n -> p j n", j=4)
         k_pool = [keep.tile([P, T * 2], BF16, name=f"k_pool{u}", align_bytes=64) for u in range(2)]
 
-        def load_pair(j, lo, hi, name):
+        def load_pair(u, lo, hi):
+            name = f"k{u}_{lo}"
             t = keep.tile([P, 2, hi - lo], F32, name=name, tag=name)
-            nc.sync.dma_start(t[:], k_view[:, j : j + 2, lo:hi])
-            return t
-
-        def cast_pair(engine_copy, pool, raw, lo, hi, base):
-            engine_copy(
-                pool[:, 2 * lo : 2 * hi].rearrange("p (n h) -> p n h", h=2),
-                raw[:, :, lo - base : hi - base].rearrange("p h n -> p n h"),
-            )
+            nc.sync.dma_start(t[:], k_view[:, 2 * u : 2 * u + 2, lo:hi])
+            return u, lo, hi, t
 
         def scalar_cast(o, i):
             nc.scalar.activation(out=o, in_=i, func=ACT.Copy)
 
-        def gather_table(row, g):
-            nc.vector.tensor_copy(g, row[:].indirect(offsets[:]))
+        def cast_pair(piece):
+            u, lo, hi, raw = piece
+            scalar_cast(
+                k_pool[u][:, 2 * lo : 2 * hi].rearrange("p (n h) -> p n h", h=2),
+                raw[:].rearrange("p h n -> p n h"),
+            )
 
-        def turn_table(g, step, name, tag):
+        def turn_table(row, step, name, tag):
+            g = keep.tile([P, N], F32, name=name + "_g")
+            nc.vector.tensor_copy(g[:], row[:].indirect(offsets[:]))
             bank = psum.tile([P, 4, P], F32, name=name + "_t", tag=tag)
             for c in range(4):
                 src = g[:, c * P : (c + 1) * P] if step == 1 else g[:, c : N : 4]
@@ -72,54 +77,53 @@ def tile_attend_x_ks_bias_srt_kernel(tc, qT, kT, vT, ks, vs, kb, offs, out):
             nc.scalar.activation(out=col[:], in_=bank[:, :, 0], func=ACT.Copy)
             return col
 
-        k0a = load_pair(0, 0, 512, "k0a")
-        nc.sync.dma_start(ks_row[0:1, :], ks[0:1, :])
-        k0b = load_pair(0, 512, T, "k0b")
+        pieces = [load_pair(0, 0, 256)]
         nc.sync.dma_start(kb_row[0:1, :], kb[0:1, :])
-        k1a = load_pair(2, 0, 512, "k1a")
-        k1b = load_pair(2, 512, T, "k1b")
+        pieces.append(load_pair(0, 256, 640))
+        nc.sync.dma_start(vs_row[0:1, :], vs[0:1, :])
+        pieces.append(load_pair(0, 640, T))
+        pieces.append(load_pair(1, 0, 384))
+        pieces.append(load_pair(1, 384, 768))
+        pieces.append(load_pair(1, 768, T))
         q_raw = keep.tile([P, 4, NQ], F32, name="q_raw", tag="q_raw")
         nc.sync.dma_start(q_raw[:], qT[0].rearrange("(p j) n -> p j n", j=4))
-        nc.sync.dma_start(vs_row[0:1, :], vs[0:1, :])
         v_raw = []
         for e in range(2):
             t = keep.tile([P, T], F32, name=f"v_raw{e}")
             nc.sync.dma_start(t[:], vT[e * P : (e + 1) * P, :])
             v_raw.append(t)
 
-        tab_g = keep.tile([P, 2, N], F32, name="tab_g", align_bytes=64)
-        gather_table(ks_row, tab_g[:, 0, :])
-        ks_bank = turn_table(tab_g[:, 0, :], 1, "ks", "x")
-        gather_table(kb_row, tab_g[:, 1, :])
-        kb_bank = turn_table(tab_g[:, 1, :], 1, "kb", "x")
+        ks_bank = turn_table(ks_row, 1, "ks", "s0")
+        kb_bank = turn_table(kb_row, 1, "kb", "s1")
+        vs_bank = turn_table(vs_row, 4, "vs", "acc0")
 
-        grp = keep.tile([P, (NQ + N) * 4], BF16, name="grp", tag="grp", align_bytes=64)
+        k_grp = keep.tile([P, N * 4], BF16, name="k_grp", align_bytes=64)
+        q_grp = keep.tile([P, NQ * 4], BF16, name="q_grp", tag="q_grp", align_bytes=64)
         codes = keep.tile([P, NQ + N], U32, name="codes", align_bytes=64)
         scales = keep.tile([P, NQ + N], U8, name="scales", align_bytes=64)
-        k_words = grp[:, NQ * 4 :].bitcast(U32).rearrange("p (i u) -> p i u", u=2)
+        k_words = k_grp[:].bitcast(U32).rearrange("p (i u) -> p i u", u=2)
 
-        cast_pair(scalar_cast, k_pool[0], k0a, 0, 512, 0)
-        cast_pair(scalar_cast, k_pool[0], k0b, 512, T, 512)
+        for piece in pieces:
+            cast_pair(piece)
         nc.vector.tensor_copy(k_words[:, :, 0], k_pool[0][:].bitcast(U32).indirect(offsets[:]))
-        cast_pair(scalar_cast, k_pool[1], k1a, 0, 512, 0)
-        cast_pair(scalar_cast, k_pool[1], k1b, 512, 704, 512)
-        cast_pair(nc.vector.tensor_copy, k_pool[1], k1b, 704, T, 512)
-        for h in range(2):
+        for h, width in ((0, 768), (1, T)):
             nc.vector.tensor_copy(
                 k_words[:, h * 256 : (h + 1) * 256, 1],
-                k_pool[1][:].bitcast(U32).indirect(offsets[:, h * 16 : (h + 1) * 16]),
+                k_pool[1][:].bitcast(U32)[:, :width].indirect(offsets[:, h * 16 : (h + 1) * 16]),
             )
-        scalar_cast(grp[:, : NQ * 4].rearrange("p (n j) -> p n j", j=4), q_raw[:].rearrange("p j n -> p n j"))
-        ks_col = column(ks_bank, "ks", "k1a")
-        kb_col = column(kb_bank, "kb", "k1b")
-        for lo, hi in ((NQ, NQ + 256), (NQ + 256, NQ + N), (0, NQ)):
+        scalar_cast(q_grp[:].rearrange("p (n j) -> p n j", j=4), q_raw[:].rearrange("p j n -> p n j"))
+        ks_col = column(ks_bank, "ks", "q_raw")
+        kb_col = column(kb_bank, "kb", "k1_768")
+        for h in range(2):
+            cols = slice(NQ + h * 256, NQ + (h + 1) * 256)
             nc.vector.quantize_mx(
-                out=codes[:, lo:hi].bitcast(FP8X4), scales=scales[:, lo:hi], in_=grp[:, lo * 4 : hi * 4]
+                out=codes[:, cols].bitcast(FP8X4), scales=scales[:, cols], in_=k_grp[:, h * 1024 : (h + 1) * 1024]
             )
+        nc.vector.quantize_mx(out=codes[:, :NQ].bitcast(FP8X4), scales=scales[:, :NQ], in_=q_grp[:])
 
         s_t = keep.tile([P, 4, NQ], F32, name="s_t")
         for c in range(4):
-            bank = psum.tile([P, NQ], F32, name="qk", tag="x" if c < 2 else "w")
+            bank = psum.tile([P, NQ], F32, name="qk", tag=f"qk{c}")
             sl = slice(NQ + c * P, NQ + (c + 1) * P)
             nc.tensor.matmul_mx(
                 out=bank[:],
@@ -134,40 +138,46 @@ def tile_attend_x_ks_bias_srt_kernel(tc, qT, kT, vT, ks, vs, kb, offs, out):
                 out=s_t[:, c, :], in_=bank[:], func=ACT.Identity,
                 scale=ks_col[:, c : c + 1], bias=kb_col[:, c : c + 1],
             )
+        vs_col = column(vs_bank, "vs", "k1_768")
 
-        g_all = keep.tile([P, 3, N], F32, name="g_all", tag="grp", align_bytes=64)
-        gather_table(vs_row, g_all[:, 0, :])
+        v_g = keep.tile([P, 2, N], BF16, name="v_g", tag="q_grp", align_bytes=64)
         for e in range(2):
-            gather_table(v_raw[e], g_all[:, 1 + e, :])
-        vs_bank = turn_table(g_all[:, 0, :], 4, "vs", "z")
-        vs_col = column(vs_bank, "vs", "k1a")
+            nc.vector.tensor_copy(
+                v_g[:, e, :].rearrange("p (u s h) -> p s u h", u=2, h=2), v_raw[e][:].indirect(offsets[:])
+            )
 
-        s_banks = []
-        for b in range(2):
-            bank = psum.tile([P, N], F32, name="s_b", tag="y")
-            for c in range(4):
-                nc.tensor.transpose(bank[:, c * P : (c + 1) * P], s_t[:, c, b * P : (b + 1) * P], ident[:])
-            s_banks.append(bank)
-        v_banks = [turn_table(g_all[:, 1 + e, :], 4, f"v{e}", "z") for e in range(2)]
+        s_banks = [psum.tile([P, N], F32, name=f"s_b{b}", tag=f"s{b}") for b in range(2)]
+        for c in range(4):
+            for b in range(2):
+                nc.tensor.transpose(s_banks[b][:, c * P : (c + 1) * P], s_t[:, c, b * P : (b + 1) * P], ident[:])
 
         neg_ms = []
+        neg_ss = []
         for b in range(2):
-            neg_m = keep.tile([P, 1], F32, name=f"neg_m{b}", tag=f"neg_m{b}", align_bytes=64)
-            nc.vector.tensor_reduce(out=neg_m[:], in_=s_banks[b][:], axis=AX.X, op=ALU.max, negate=True)
+            neg_m = keep.tile([P, 1], F32, name=f"neg_m{b}")
+            neg_s = keep.tile([P, 4, P], F32, name=f"neg_s{b}")
+            nc.vector.tensor_scalar(
+                out=neg_s[:], in0=s_banks[b][:].rearrange("p (s t) -> p t s", t=4),
+                scalar1=-1.0, scalar2=None, op0=ALU.mult, op1=ALU.min, accum_out=neg_m[:],
+            )
             neg_ms.append(neg_m)
+            neg_ss.append(neg_s)
+        v_bank = psum.tile([P, 2, 2, P], F32, name="v_t", tag="s0")
+        v_words = v_g[:].rearrange("p e n -> p (e n)").bitcast(F32)
+        for e in range(2):
+            for u in range(2):
+                lo = (2 * e + u) * P
+                nc.tensor.transpose(v_bank[:, e, u, :], v_words[:, lo : lo + P], ident[:])
+
         v_codes = keep.tile([P, DV], U32, name="v_codes", align_bytes=64)
         v_scale = keep.tile([P, DV], U8, name="v_scale", align_bytes=64)
+        v_grp = keep.tile([P, DV * 4], BF16, name="v_grp", align_bytes=64)
+        nc.vector.tensor_copy(
+            v_grp[:].bitcast(F32).rearrange("p (e r u) -> p e r u", e=2, u=2),
+            v_bank[:].rearrange("p e u r -> p e r u"),
+        )
+        nc.vector.quantize_mx(out=v_codes[:].bitcast(FP8X4), scales=v_scale[:], in_=v_grp[:])
 
-        def value_group(engine_copy, bank, e, tag):
-            v_grp = keep.tile([P, P * 4], BF16, name=f"v_grp{e}", tag=tag, align_bytes=64)
-            engine_copy(v_grp[:].rearrange("p (e t) -> p e t", t=4), bank[:].rearrange("p t e -> p e t"))
-            return v_grp
-
-        def quantize_values(v_grp, e):
-            cols = slice(e * P, (e + 1) * P)
-            nc.vector.quantize_mx(out=v_codes[:, cols].bitcast(FP8X4), scales=v_scale[:, cols], in_=v_grp[:])
-
-        quantize_values(value_group(nc.vector.tensor_copy, v_banks[0], 0, "v_grp0"), 0)
         p_tiles = []
         l_tiles = []
         for b in range(2):
@@ -175,17 +185,18 @@ def tile_attend_x_ks_bias_srt_kernel(tc, qT, kT, vT, ks, vs, kb, offs, out):
             l = keep.tile([P, 1], F32, name=f"l{b}")
             nc.scalar.activation(
                 out=p[:],
-                in_=s_banks[b][:].rearrange("p (s t) -> p t s", t=4),
+                in_=neg_ss[b][:],
                 func=ACT.Exp,
+                scale=-1.0,
                 bias=neg_ms[b][:],
                 accum_out=l[:],
             )
             p_tiles.append(p)
             l_tiles.append(l)
-        v_grp1 = value_group(scalar_cast, v_banks[1], 1, "neg_m1")
 
+        w_grps = []
         for b in range(2):
-            bank = psum.tile([P, 4, P], F32, name="p_t", tag="x")
+            bank = psum.tile([P, 4, P], F32, name="p_t", tag=f"qk{b}")
             for t in range(4):
                 nc.tensor.transpose(bank[:, t, :], p_tiles[b][:, t, :], ident[:])
             w_grp = keep.tile([P, P * 4], BF16, name=f"w_grp{b}", align_bytes=64)
@@ -195,14 +206,14 @@ def tile_attend_x_ks_bias_srt_kernel(tc, qT, kT, vT, ks, vs, kb, offs, out):
                 in1=vs_col[:].unsqueeze(1).to_broadcast([P, P, 4]),
                 op=ALU.mult,
             )
+            w_grps.append(w_grp)
+        for b in range(2):
             w_codes = keep.tile([P, P], U32, name=f"w_codes{b}", align_bytes=64)
             w_scale = keep.tile([P, P], U8, name=f"w_scale{b}", align_bytes=64)
-            nc.vector.quantize_mx(out=w_codes[:].bitcast(FP8X4), scales=w_scale[:], in_=w_grp[:])
-            if b == 0:
-                quantize_values(v_grp1, 1)
+            nc.vector.quantize_mx(out=w_codes[:].bitcast(FP8X4), scales=w_scale[:], in_=w_grps[b][:])
             rl = keep.tile([P, 1], F32, name=f"rl{b}")
             nc.vector.reciprocal(rl[:], l_tiles[b][:])
-            acc = psum.tile([P, DV], F32, name="acc", tag="w")
+            acc = psum.tile([P, DV], F32, name="acc", tag=f"acc{b}")
             nc.tensor.matmul_mx(
                 out=acc[:],
                 lhsT=w_codes[:].bitcast(FP8X4),

@@ -4,6 +4,7 @@ import concourse.mybir as mybir
 from concourse.masks import make_identity
 
 P = 128
+LAST = P - 1
 D, T, N, NQ, DV = 512, 1024, 512, 256, 256
 F32 = mybir.dt.float32
 BF16 = mybir.dt.bfloat16
@@ -33,23 +34,23 @@ def tile_attend_x_ks_bias_srt_kernel(tc, qT, kT, vT, ks, vs, kb, offs, out):
         ident = keep.tile([P, P], F32, name="ident")
 
         nc.sync.dma_start(offsets[:], offs)
-        nc.sync.dma_start(ks_row[0:32, :], ks[0:32, :])
-        nc.gpsimd.memset(kb_row[:, :512], 0.0)
-        nc.vector.memset(kb_row[:, 512:], 0.0)
+        nc.scalar.dma_start(ks_row[LAST:, :], ks[LAST:, :])
+        nc.scalar.dma_start(kb_row[LAST:, :], kb[LAST:, :])
+        nc.scalar.dma_start(vs_row[LAST:, :], vs[LAST:, :])
         nc.vector.memset(warm[:], 0.0)
         nc.scalar.activation(out=warm[:], in_=warm[:], func=ACT.Exp)
-        nc.gpsimd.memset(vs_row[:, :512], 0.0)
-        nc.vector.memset(vs_row[:, 512:], 0.0)
-        nc.gpsimd.memset(ks_row[32:64, :], 0.0)
-        nc.vector.memset(ks_row[64:128, :], 0.0)
+        for row in (ks_row, kb_row):
+            nc.gpsimd.memset(row[:LAST, :384], 0.0)
+            nc.vector.memset(row[:LAST, 384:], 0.0)
         make_identity(nc, ident[:])
+        nc.gpsimd.memset(vs_row[:LAST, :], 0.0)
 
         k_view = kT.rearrange("(p j) n -> p j n", j=4)
         k_pool = [keep.tile([P, T * 2], BF16, name=f"k_pool{u}", align_bytes=64) for u in range(2)]
 
         def load_pair(u, lo, hi):
             name = f"k{u}_{lo}"
-            t = keep.tile([P, 2, hi - lo], F32, name=name, tag=name)
+            t = keep.tile([P, 2, hi - lo], F32, name=name, tag=name, align_bytes=64)
             nc.sync.dma_start(t[:], k_view[:, 2 * u : 2 * u + 2, lo:hi])
             return u, lo, hi, t
 
@@ -72,15 +73,11 @@ def tile_attend_x_ks_bias_srt_kernel(tc, qT, kT, vT, ks, vs, kb, offs, out):
                 nc.tensor.transpose(bank[:, c, :], src, ident[:])
             return bank
 
-        def column(bank, name, tag):
-            col = keep.tile([P, 4], F32, name=name + "_c", tag=tag)
-            nc.scalar.activation(out=col[:], in_=bank[:, :, 0], func=ACT.Copy)
-            return col
+        def column(bank, col):
+            nc.scalar.activation(out=col, in_=bank[:, :, LAST], func=ACT.Copy)
 
         pieces = [load_pair(0, 0, 256)]
-        nc.sync.dma_start(kb_row[0:1, :], kb[0:1, :])
         pieces.append(load_pair(0, 256, 640))
-        nc.sync.dma_start(vs_row[0:1, :], vs[0:1, :])
         pieces.append(load_pair(0, 640, T))
         pieces.append(load_pair(1, 0, 384))
         pieces.append(load_pair(1, 384, 768))
@@ -99,8 +96,9 @@ def tile_attend_x_ks_bias_srt_kernel(tc, qT, kT, vT, ks, vs, kb, offs, out):
 
         k_grp = keep.tile([P, N * 4], BF16, name="k_grp", align_bytes=64)
         q_grp = keep.tile([P, NQ * 4], BF16, name="q_grp", tag="q_grp", align_bytes=64)
-        codes = keep.tile([P, NQ + N], U32, name="codes", align_bytes=64)
-        scales = keep.tile([P, NQ + N], U8, name="scales", align_bytes=64)
+        q_codes = keep.tile([P, NQ], U32, name="q_codes", align_bytes=64)
+        q_scale = keep.tile([P, NQ], U8, name="q_scale", align_bytes=64)
+        k_scale = keep.tile([P, N], U8, name="k_scale", align_bytes=64)
         k_words = k_grp[:].bitcast(U32).rearrange("p (i u) -> p i u", u=2)
 
         for piece in pieces:
@@ -112,33 +110,36 @@ def tile_attend_x_ks_bias_srt_kernel(tc, qT, kT, vT, ks, vs, kb, offs, out):
                 k_pool[1][:].bitcast(U32)[:, :width].indirect(offsets[:, h * 16 : (h + 1) * 16]),
             )
         scalar_cast(q_grp[:].rearrange("p (n j) -> p n j", j=4), q_raw[:].rearrange("p j n -> p n j"))
-        ks_col = column(ks_bank, "ks", "q_raw")
-        kb_col = column(kb_bank, "kb", "k1_768")
+        k_cols = keep.tile([P, 2, 4], F32, name="k_cols", tag="q_raw")
+        column(ks_bank, k_cols[:, 0, :])
+        column(kb_bank, k_cols[:, 1, :])
+        k_codes = keep.tile([P, N], U32, name="k_codes", tag="k1_768", align_bytes=64)
         for h in range(2):
-            cols = slice(NQ + h * 256, NQ + (h + 1) * 256)
+            cols = slice(h * 256, (h + 1) * 256)
             nc.vector.quantize_mx(
-                out=codes[:, cols].bitcast(FP8X4), scales=scales[:, cols], in_=k_grp[:, h * 1024 : (h + 1) * 1024]
+                out=k_codes[:, cols].bitcast(FP8X4), scales=k_scale[:, cols], in_=k_grp[:, h * 1024 : (h + 1) * 1024]
             )
-        nc.vector.quantize_mx(out=codes[:, :NQ].bitcast(FP8X4), scales=scales[:, :NQ], in_=q_grp[:])
+        nc.vector.quantize_mx(out=q_codes[:].bitcast(FP8X4), scales=q_scale[:], in_=q_grp[:])
 
         s_t = keep.tile([P, 4, NQ], F32, name="s_t")
         for c in range(4):
             bank = psum.tile([P, NQ], F32, name="qk", tag=f"qk{c}")
-            sl = slice(NQ + c * P, NQ + (c + 1) * P)
+            sl = slice(c * P, (c + 1) * P)
             nc.tensor.matmul_mx(
                 out=bank[:],
-                lhsT=codes[:, sl].bitcast(FP8X4),
-                lhsT_scale=scales[:, sl],
-                rhs=codes[:, :NQ].bitcast(FP8X4),
-                rhs_scale=scales[:, :NQ],
+                lhsT=k_codes[:, sl].bitcast(FP8X4),
+                lhsT_scale=k_scale[:, sl],
+                rhs=q_codes[:].bitcast(FP8X4),
+                rhs_scale=q_scale[:],
                 start=True,
                 stop=True,
             )
             nc.scalar.activation(
                 out=s_t[:, c, :], in_=bank[:], func=ACT.Identity,
-                scale=ks_col[:, c : c + 1], bias=kb_col[:, c : c + 1],
+                scale=k_cols[:, 0, c : c + 1], bias=k_cols[:, 1, c : c + 1],
             )
-        vs_col = column(vs_bank, "vs", "k1_768")
+        vs_col = keep.tile([P, 4], F32, name="vs_col", tag="q_raw")
+        column(vs_bank, vs_col[:])
 
         v_g = keep.tile([P, 2, N], BF16, name="v_g", tag="q_grp", align_bytes=64)
         for e in range(2):
@@ -151,6 +152,21 @@ def tile_attend_x_ks_bias_srt_kernel(tc, qT, kT, vT, ks, vs, kb, offs, out):
             for b in range(2):
                 nc.tensor.transpose(s_banks[b][:, c * P : (c + 1) * P], s_t[:, c, b * P : (b + 1) * P], ident[:])
 
+        v_codes = keep.tile([P, DV], U32, name="v_codes", align_bytes=64)
+        v_scale = keep.tile([P, DV], U8, name="v_scale", align_bytes=64)
+        v_words = v_g[:].rearrange("p e n -> p (e n)").bitcast(F32)
+
+        def value_half(e, tag, engine_copy):
+            bank = psum.tile([P, 2, P], F32, name=f"v_t{e}", tag=tag)
+            for u in range(2):
+                lo = (2 * e + u) * P
+                nc.tensor.transpose(bank[:, u, :], v_words[:, lo : lo + P], ident[:])
+            v_grp = keep.tile([P, P * 4], BF16, name=f"v_grp{e}", align_bytes=64)
+            engine_copy(v_grp[:].bitcast(F32).rearrange("p (r u) -> p r u", u=2), bank[:].rearrange("p u r -> p r u"))
+            cols = slice(e * P, (e + 1) * P)
+            nc.vector.quantize_mx(out=v_codes[:, cols].bitcast(FP8X4), scales=v_scale[:, cols], in_=v_grp[:])
+
+        value_half(0, "qk2", nc.scalar.copy)
         neg_ms = []
         neg_ss = []
         for b in range(2):
@@ -162,21 +178,7 @@ def tile_attend_x_ks_bias_srt_kernel(tc, qT, kT, vT, ks, vs, kb, offs, out):
             )
             neg_ms.append(neg_m)
             neg_ss.append(neg_s)
-        v_bank = psum.tile([P, 2, 2, P], F32, name="v_t", tag="s0")
-        v_words = v_g[:].rearrange("p e n -> p (e n)").bitcast(F32)
-        for e in range(2):
-            for u in range(2):
-                lo = (2 * e + u) * P
-                nc.tensor.transpose(v_bank[:, e, u, :], v_words[:, lo : lo + P], ident[:])
-
-        v_codes = keep.tile([P, DV], U32, name="v_codes", align_bytes=64)
-        v_scale = keep.tile([P, DV], U8, name="v_scale", align_bytes=64)
-        v_grp = keep.tile([P, DV * 4], BF16, name="v_grp", align_bytes=64)
-        nc.vector.tensor_copy(
-            v_grp[:].bitcast(F32).rearrange("p (e r u) -> p e r u", e=2, u=2),
-            v_bank[:].rearrange("p e u r -> p e r u"),
-        )
-        nc.vector.quantize_mx(out=v_codes[:].bitcast(FP8X4), scales=v_scale[:], in_=v_grp[:])
+        value_half(1, "s0", nc.vector.tensor_copy)
 
         p_tiles = []
         l_tiles = []

@@ -109,7 +109,9 @@ def tile_attend_x_ks_bias_srt_kernel(tc, qT, kT, vT, ks, vs, kb, offs, out):
                 k_words[:, h * 256 : (h + 1) * 256, 1],
                 k_pool[1][:].bitcast(U32)[:, :width].indirect(offsets[:, h * 16 : (h + 1) * 16]),
             )
-        scalar_cast(q_grp[:].rearrange("p (n j) -> p n j", j=4), q_raw[:].rearrange("p j n -> p n j"))
+        scalar_cast(
+            q_grp[:].rearrange("p (c i j) -> p c j i", i=4, j=4), q_raw[:].rearrange("p j (c i) -> p c j i", i=4)
+        )
         k_cols = keep.tile([P, 2, 4], F32, name="k_cols", tag="q_raw")
         column(ks_bank, k_cols[:, 0, :])
         column(kb_bank, k_cols[:, 1, :])
@@ -181,20 +183,19 @@ def tile_attend_x_ks_bias_srt_kernel(tc, qT, kT, vT, ks, vs, kb, offs, out):
         value_half(1, "s0", nc.vector.tensor_copy)
 
         p_tiles = []
-        l_tiles = []
+        l_parts = keep.tile([P, 2, 2], F32, name="l_parts")
         for b in range(2):
             p = keep.tile([P, 4, P], F32, name=f"p{b}")
-            l = keep.tile([P, 1], F32, name=f"l{b}")
-            nc.scalar.activation(
-                out=p[:],
-                in_=neg_ss[b][:],
-                func=ACT.Exp,
-                scale=-1.0,
-                bias=neg_ms[b][:],
-                accum_out=l[:],
-            )
+            for h in range(2):
+                nc.scalar.activation(
+                    out=p[:, 2 * h : 2 * h + 2, :],
+                    in_=neg_ss[b][:, 2 * h : 2 * h + 2, :],
+                    func=ACT.Exp,
+                    scale=-1.0,
+                    bias=neg_ms[b][:],
+                    accum_out=l_parts[:, h, b : b + 1],
+                )
             p_tiles.append(p)
-            l_tiles.append(l)
 
         w_grps = []
         for b in range(2):
@@ -209,22 +210,28 @@ def tile_attend_x_ks_bias_srt_kernel(tc, qT, kT, vT, ks, vs, kb, offs, out):
                 op=ALU.mult,
             )
             w_grps.append(w_grp)
+        l_sum = keep.tile([P, 2], F32, name="l_sum")
+        rl = keep.tile([P, 2], F32, name="rl")
+        nc.vector.tensor_tensor(out=l_sum[:], in0=l_parts[:, 0, :], in1=l_parts[:, 1, :], op=ALU.add)
+        nc.vector.reciprocal(rl[:], l_sum[:])
         for b in range(2):
             w_codes = keep.tile([P, P], U32, name=f"w_codes{b}", align_bytes=64)
             w_scale = keep.tile([P, P], U8, name=f"w_scale{b}", align_bytes=64)
             nc.vector.quantize_mx(out=w_codes[:].bitcast(FP8X4), scales=w_scale[:], in_=w_grps[b][:])
-            rl = keep.tile([P, 1], F32, name=f"rl{b}")
-            nc.vector.reciprocal(rl[:], l_tiles[b][:])
-            acc = psum.tile([P, DV], F32, name="acc", tag=f"acc{b}")
-            nc.tensor.matmul_mx(
-                out=acc[:],
-                lhsT=w_codes[:].bitcast(FP8X4),
-                lhsT_scale=w_scale[:],
-                rhs=v_codes[:].bitcast(FP8X4),
-                rhs_scale=v_scale[:],
-                start=True,
-                stop=True,
-            )
             y = keep.tile([P, DV], F32, name=f"y{b}")
-            nc.scalar.activation(out=y[:], in_=acc[:], func=ACT.Copy, scale=rl[:])
+            for lo, hi, tag in ((0, P, f"acc{b}"), (P, DV, f"s{b}")):
+                acc = psum.tile([P, hi - lo], F32, name="acc", tag=tag)
+                nc.tensor.matmul_mx(
+                    out=acc[:],
+                    lhsT=w_codes[:].bitcast(FP8X4),
+                    lhsT_scale=w_scale[:],
+                    rhs=v_codes[:, lo:hi].bitcast(FP8X4),
+                    rhs_scale=v_scale[:, lo:hi],
+                    start=True,
+                    stop=True,
+                )
+                if lo == 0:
+                    nc.scalar.activation(out=y[:, lo:hi], in_=acc[:], func=ACT.Copy, scale=rl[:, b : b + 1])
+                else:
+                    nc.vector.tensor_scalar(out=y[:, lo:hi], in0=acc[:], scalar1=rl[:, b : b + 1], scalar2=None, op0=ALU.mult)
             nc.sync.dma_start(out[0, b * P : (b + 1) * P, :], y[:])

@@ -24,6 +24,7 @@ def tile_attend_x_ks_bias_srt_kernel(tc, qT, kT, vT, ks, vs, kb, offs, out):
     nc = tc.nc
     with ExitStack() as ctx:
         keep = ctx.enter_context(tc.tile_pool(name="keep", bufs=1))
+        shared = ctx.enter_context(tc.tile_pool(name="shared", bufs=1))
         psum = ctx.enter_context(tc.psum_pool(name="psum", bufs=1))
 
         offsets = keep.tile([P, N // 16], U16, name="offsets")
@@ -82,7 +83,7 @@ def tile_attend_x_ks_bias_srt_kernel(tc, qT, kT, vT, ks, vs, kb, offs, out):
         pieces.append(load_pair(1, 0, 384))
         pieces.append(load_pair(1, 384, 768))
         pieces.append(load_pair(1, 768, T))
-        q_raw = keep.tile([P, 4, NQ], F32, name="q_raw", tag="q_raw")
+        q_raw = shared.tile([P, 4, NQ], F32, name="q_raw", offset=0, align_bytes=64)
         nc.sync.dma_start(q_raw[:], qT[0].rearrange("(p j) n -> p j n", j=4))
         v_raw = []
         for e in range(2):
@@ -109,49 +110,59 @@ def tile_attend_x_ks_bias_srt_kernel(tc, qT, kT, vT, ks, vs, kb, offs, out):
                 k_words[:, h * 256 : (h + 1) * 256, 1],
                 k_pool[1][:].bitcast(U32)[:, :width].indirect(offsets[:, h * 16 : (h + 1) * 16]),
             )
-        scalar_cast(
-            q_grp[:].rearrange("p (c i j) -> p c j i", i=4, j=4), q_raw[:].rearrange("p j (c i) -> p c j i", i=4)
-        )
-        k_cols = keep.tile([P, 2, 4], F32, name="k_cols", tag="q_raw")
-        column(ks_bank, k_cols[:, 0, :])
-        column(kb_bank, k_cols[:, 1, :])
+        for b in range(2):
+            scalar_cast(
+                q_grp[:, 4 * b * P : 4 * (b + 1) * P].rearrange("p (c i j) -> p c j i", i=4, j=4),
+                q_raw[:, :, b * P : (b + 1) * P].rearrange("p j (c i) -> p c j i", i=4),
+            )
+        k_cols = shared.tile([P, 2, 16], F32, name="k_cols", offset=0, align_bytes=64)
+        column(ks_bank, k_cols[:, 0, :4])
+        column(kb_bank, k_cols[:, 1, :4])
         k_codes = keep.tile([P, N], U32, name="k_codes", tag="k1_768", align_bytes=64)
         for h in range(2):
             cols = slice(h * 256, (h + 1) * 256)
             nc.vector.quantize_mx(
                 out=k_codes[:, cols].bitcast(FP8X4), scales=k_scale[:, cols], in_=k_grp[:, h * 1024 : (h + 1) * 1024]
             )
-        nc.vector.quantize_mx(out=q_codes[:].bitcast(FP8X4), scales=q_scale[:], in_=q_grp[:])
+            cols = slice(h * P, (h + 1) * P)
+            nc.vector.quantize_mx(
+                out=q_codes[:, cols].bitcast(FP8X4), scales=q_scale[:, cols], in_=q_grp[:, h * 512 : (h + 1) * 512]
+            )
 
         s_t = keep.tile([P, 4, NQ], F32, name="s_t")
-        for c in range(4):
-            bank = psum.tile([P, NQ], F32, name="qk", tag=f"qk{c}")
-            sl = slice(c * P, (c + 1) * P)
-            nc.tensor.matmul_mx(
-                out=bank[:],
-                lhsT=k_codes[:, sl].bitcast(FP8X4),
-                lhsT_scale=k_scale[:, sl],
-                rhs=q_codes[:].bitcast(FP8X4),
-                rhs_scale=q_scale[:],
-                start=True,
-                stop=True,
-            )
-            nc.scalar.activation(
-                out=s_t[:, c, :], in_=bank[:], func=ACT.Identity,
-                scale=k_cols[:, 0, c : c + 1], bias=k_cols[:, 1, c : c + 1],
-            )
-        vs_col = keep.tile([P, 4], F32, name="vs_col", tag="q_raw")
+        for b in range(2):
+            q_cols = slice(b * P, (b + 1) * P)
+            for h in range(2):
+                bank = psum.tile([P, 2, P], F32, name="qk", tag=f"qk{2 * b + h}")
+                for i in range(2):
+                    sl = slice((2 * h + i) * P, (2 * h + i + 1) * P)
+                    nc.tensor.matmul_mx(
+                        out=bank[:, i, :],
+                        lhsT=k_codes[:, sl].bitcast(FP8X4),
+                        lhsT_scale=k_scale[:, sl],
+                        rhs=q_codes[:, q_cols].bitcast(FP8X4),
+                        rhs_scale=q_scale[:, q_cols],
+                        start=True,
+                        stop=True,
+                    )
+                for i in range(2):
+                    c = 2 * h + i
+                    nc.scalar.activation(
+                        out=s_t[:, c, q_cols], in_=bank[:, i, :], func=ACT.Identity,
+                        scale=k_cols[:, 0, c : c + 1], bias=k_cols[:, 1, c : c + 1],
+                    )
+        vs_col = shared.tile([P, 4], F32, name="vs_col", offset=0, align_bytes=64)
         column(vs_bank, vs_col[:])
 
-        v_g = keep.tile([P, 2, N], BF16, name="v_g", tag="q_grp", align_bytes=64)
+        v_g = shared.tile([P, 2, N], BF16, name="v_g", offset=2112, align_bytes=64)
         for e in range(2):
             nc.vector.tensor_copy(
                 v_g[:, e, :].rearrange("p (u s h) -> p s u h", u=2, h=2), v_raw[e][:].indirect(offsets[:])
             )
 
         s_banks = [psum.tile([P, N], F32, name=f"s_b{b}", tag=f"s{b}") for b in range(2)]
-        for c in range(4):
-            for b in range(2):
+        for b in range(2):
+            for c in range(4):
                 nc.tensor.transpose(s_banks[b][:, c * P : (c + 1) * P], s_t[:, c, b * P : (b + 1) * P], ident[:])
 
         v_codes = keep.tile([P, DV], U32, name="v_codes", align_bytes=64)
@@ -163,35 +174,31 @@ def tile_attend_x_ks_bias_srt_kernel(tc, qT, kT, vT, ks, vs, kb, offs, out):
             for u in range(2):
                 lo = (2 * e + u) * P
                 nc.tensor.transpose(bank[:, u, :], v_words[:, lo : lo + P], ident[:])
-            v_grp = keep.tile([P, P * 4], BF16, name=f"v_grp{e}", align_bytes=64)
+            v_grp = shared.tile([P, P * 4], BF16, name=f"v_grp{e}", offset=64 + 1024 * e, align_bytes=64)
             engine_copy(v_grp[:].bitcast(F32).rearrange("p (r u) -> p r u", u=2), bank[:].rearrange("p u r -> p r u"))
             cols = slice(e * P, (e + 1) * P)
             nc.vector.quantize_mx(out=v_codes[:, cols].bitcast(FP8X4), scales=v_scale[:, cols], in_=v_grp[:])
 
-        value_half(0, "qk2", nc.scalar.copy)
-        neg_ms = []
-        neg_ss = []
-        for b in range(2):
-            neg_m = keep.tile([P, 1], F32, name=f"neg_m{b}")
-            neg_s = keep.tile([P, 4, P], F32, name=f"neg_s{b}")
-            nc.vector.tensor_scalar(
-                out=neg_s[:], in0=s_banks[b][:].rearrange("p (s t) -> p t s", t=4),
-                scalar1=-1.0, scalar2=None, op0=ALU.mult, op1=ALU.min, accum_out=neg_m[:],
-            )
-            neg_ms.append(neg_m)
-            neg_ss.append(neg_s)
+        value_half(0, "acc1", nc.scalar.copy)
+        neg_ms = [keep.tile([P, 1], F32, name=f"neg_m{b}") for b in range(2)]
+        dealt = [bank[:].rearrange("p (s t) -> p t s", t=4) for bank in s_banks]
+        neg_s = keep.tile([P, 4, P], F32, name="neg_s")
+        nc.vector.tensor_scalar(
+            out=neg_s[:], in0=dealt[0], scalar1=-1.0, scalar2=None, op0=ALU.mult, op1=ALU.min, accum_out=neg_ms[0][:]
+        )
+        nc.vector.tensor_reduce(out=neg_ms[1][:], in_=s_banks[1][:], axis=AX.X, op=ALU.max, negate=True)
         value_half(1, "s0", nc.vector.tensor_copy)
 
         p_tiles = []
         l_parts = keep.tile([P, 2, 2], F32, name="l_parts")
-        for b in range(2):
+        for b, (scores, sign) in enumerate(((neg_s[:], -1.0), (dealt[1], 1.0))):
             p = keep.tile([P, 4, P], F32, name=f"p{b}")
             for h in range(2):
                 nc.scalar.activation(
                     out=p[:, 2 * h : 2 * h + 2, :],
-                    in_=neg_ss[b][:, 2 * h : 2 * h + 2, :],
+                    in_=scores[:, 2 * h : 2 * h + 2, :],
                     func=ACT.Exp,
-                    scale=-1.0,
+                    scale=sign,
                     bias=neg_ms[b][:],
                     accum_out=l_parts[:, h, b : b + 1],
                 )

@@ -6,6 +6,8 @@ from concourse.masks import make_identity
 P = 128
 LAST = P - 1
 D, T, N, NQ, DV = 512, 1024, 512, 256, 256
+HALF = N // 2
+PREFIX = T - HALF
 F32 = mybir.dt.float32
 BF16 = mybir.dt.bfloat16
 U32 = mybir.dt.uint32
@@ -15,6 +17,12 @@ FP8X4 = mybir.dt.float8_e4m3fn_x4
 ACT = mybir.ActivationFunctionType
 ALU = mybir.AluOpType
 AX = mybir.AxisListType
+
+KEY_CUTS = ((0, 256, 640, T), (0, 384, PREFIX, T))
+GPSIMD_CLEARS = 384
+V_GRP_AT = 64
+V_HALF_BYTES = 1024
+V_G_AT = V_GRP_AT + 2 * V_HALF_BYTES
 
 FLOPS = 2 * NQ * N * (D + DV)
 BYTES = 4 * (D * NQ + (D + DV) * N + 3 * N + NQ * DV) + 2 * N
@@ -27,218 +35,193 @@ def tile_attend_x_ks_bias_srt_kernel(tc, qT, kT, vT, ks, vs, kb, offs, out):
         shared = ctx.enter_context(tc.tile_pool(name="shared", bufs=1))
         psum = ctx.enter_context(tc.psum_pool(name="psum", bufs=1))
 
+        def block(i, width=P):
+            return slice(i * width, (i + 1) * width)
+
+        def scalar_cast(dst, src):
+            nc.scalar.activation(out=dst, in_=src, func=ACT.Copy)
+
+        def quantize(codes, scales, cols, grouped):
+            nc.vector.quantize_mx(out=codes[:, cols].bitcast(FP8X4), scales=scales[:, cols], in_=grouped)
+
+        def product(acc, lhs_codes, lhs_scales, lhs_cols, rhs_codes, rhs_scales, rhs_cols):
+            nc.tensor.matmul_mx(
+                out=acc,
+                lhsT=lhs_codes[:, lhs_cols].bitcast(FP8X4),
+                lhsT_scale=lhs_scales[:, lhs_cols],
+                rhs=rhs_codes[:, rhs_cols].bitcast(FP8X4),
+                rhs_scale=rhs_scales[:, rhs_cols],
+                start=True,
+                stop=True,
+            )
+
         offsets = keep.tile([P, N // 16], U16, name="offsets")
         ks_row = keep.tile([P, T], F32, name="ks_row")
         kb_row = keep.tile([P, T], F32, name="kb_row")
         vs_row = keep.tile([P, T], F32, name="vs_row")
-        warm = keep.tile([P, 1], F32, name="warm")
         ident = keep.tile([P, P], F32, name="ident")
-
         nc.sync.dma_start(offsets[:], offs)
-        nc.scalar.dma_start(ks_row[LAST:, :], ks[LAST:, :])
-        nc.scalar.dma_start(kb_row[LAST:, :], kb[LAST:, :])
-        nc.scalar.dma_start(vs_row[LAST:, :], vs[LAST:, :])
-        nc.vector.memset(warm[:], 0.0)
-        nc.scalar.activation(out=warm[:], in_=warm[:], func=ACT.Exp)
+        for row, table in ((ks_row, ks), (kb_row, kb), (vs_row, vs)):
+            nc.scalar.dma_start(row[LAST:, :], table[LAST:, :])
         for row in (ks_row, kb_row):
-            nc.gpsimd.memset(row[:LAST, :384], 0.0)
-            nc.vector.memset(row[:LAST, 384:], 0.0)
+            nc.gpsimd.memset(row[:LAST, :GPSIMD_CLEARS], 0.0)
+            nc.vector.memset(row[:LAST, GPSIMD_CLEARS:], 0.0)
         make_identity(nc, ident[:])
         nc.gpsimd.memset(vs_row[:LAST, :], 0.0)
 
-        k_view = kT.rearrange("(p j) n -> p j n", j=4)
+        k_planes = kT.rearrange("(p j) n -> p j n", j=4)
         k_pool = [keep.tile([P, T * 2], BF16, name=f"k_pool{u}", align_bytes=64) for u in range(2)]
-
-        def load_pair(u, lo, hi):
-            name = f"k{u}_{lo}"
-            t = keep.tile([P, 2, hi - lo], F32, name=name, tag=name, align_bytes=64)
-            nc.sync.dma_start(t[:], k_view[:, 2 * u : 2 * u + 2, lo:hi])
-            return u, lo, hi, t
-
-        def scalar_cast(o, i):
-            nc.scalar.activation(out=o, in_=i, func=ACT.Copy)
-
-        def cast_pair(piece):
-            u, lo, hi, raw = piece
-            scalar_cast(
-                k_pool[u][:, 2 * lo : 2 * hi].rearrange("p (n h) -> p n h", h=2),
-                raw[:].rearrange("p h n -> p n h"),
-            )
-
-        def turn_table(row, step, name, tag):
-            g = keep.tile([P, N], F32, name=name + "_g")
-            nc.vector.tensor_copy(g[:], row[:].indirect(offsets[:]))
-            bank = psum.tile([P, 4, P], F32, name=name + "_t", tag=tag)
-            for c in range(4):
-                src = g[:, c * P : (c + 1) * P] if step == 1 else g[:, c : N : 4]
-                nc.tensor.transpose(bank[:, c, :], src, ident[:])
-            return bank
-
-        def column(bank, col):
-            nc.scalar.activation(out=col, in_=bank[:, :, LAST], func=ACT.Copy)
-
-        pieces = [load_pair(0, 0, 256)]
-        pieces.append(load_pair(0, 256, 640))
-        pieces.append(load_pair(0, 640, T))
-        pieces.append(load_pair(1, 0, 384))
-        pieces.append(load_pair(1, 384, 768))
-        pieces.append(load_pair(1, 768, T))
+        pieces = []
+        for u, cuts in enumerate(KEY_CUTS):
+            for lo, hi in zip(cuts, cuts[1:]):
+                raw = keep.tile([P, 2, hi - lo], F32, name=f"k{u}_{lo}", tag=f"k{u}_{lo}", align_bytes=64)
+                nc.sync.dma_start(raw[:], k_planes[:, 2 * u : 2 * u + 2, lo:hi])
+                pieces.append((u, lo, hi, raw))
         q_raw = shared.tile([P, 4, NQ], F32, name="q_raw", offset=0, align_bytes=64)
         nc.sync.dma_start(q_raw[:], qT[0].rearrange("(p j) n -> p j n", j=4))
-        v_raw = []
+        v_raw = [keep.tile([P, T], F32, name=f"v_raw{e}") for e in range(2)]
         for e in range(2):
-            t = keep.tile([P, T], F32, name=f"v_raw{e}")
-            nc.sync.dma_start(t[:], vT[e * P : (e + 1) * P, :])
-            v_raw.append(t)
+            nc.sync.dma_start(v_raw[e][:], vT[block(e), :])
 
-        ks_bank = turn_table(ks_row, 1, "ks", "s0")
-        kb_bank = turn_table(kb_row, 1, "kb", "s1")
-        vs_bank = turn_table(vs_row, 4, "vs", "acc0")
+        def turn_table(row, name, tag, slots):
+            gathered = keep.tile([P, N], F32, name=name + "_g")
+            nc.vector.tensor_copy(gathered[:], row[:].indirect(offsets[:]))
+            bank = psum.tile([P, 4, P], F32, name=name + "_t", tag=tag)
+            for c in range(4):
+                nc.tensor.transpose(bank[:, c, :], gathered[:, slots(c)], ident[:])
+            return bank
+
+        ks_bank = turn_table(ks_row, "ks", "s0", block)
+        kb_bank = turn_table(kb_row, "kb", "s1", block)
+        vs_bank = turn_table(vs_row, "vs", "acc0", lambda t: slice(t, N, 4))
 
         k_grp = keep.tile([P, N * 4], BF16, name="k_grp", align_bytes=64)
-        q_grp = keep.tile([P, NQ * 4], BF16, name="q_grp", tag="q_grp", align_bytes=64)
+        q_grp = keep.tile([P, NQ * 4], BF16, name="q_grp", align_bytes=64)
         q_codes = keep.tile([P, NQ], U32, name="q_codes", align_bytes=64)
         q_scale = keep.tile([P, NQ], U8, name="q_scale", align_bytes=64)
         k_scale = keep.tile([P, N], U8, name="k_scale", align_bytes=64)
         k_words = k_grp[:].bitcast(U32).rearrange("p (i u) -> p i u", u=2)
-
-        for piece in pieces:
-            cast_pair(piece)
-        nc.vector.tensor_copy(k_words[:, :, 0], k_pool[0][:].bitcast(U32).indirect(offsets[:]))
-        for h, width in ((0, 768), (1, T)):
-            nc.vector.tensor_copy(
-                k_words[:, h * 256 : (h + 1) * 256, 1],
-                k_pool[1][:].bitcast(U32)[:, :width].indirect(offsets[:, h * 16 : (h + 1) * 16]),
+        for u, lo, hi, raw in pieces:
+            scalar_cast(
+                k_pool[u][:, 2 * lo : 2 * hi].rearrange("p (n h) -> p n h", h=2), raw[:].rearrange("p h n -> p n h")
             )
+        nc.vector.tensor_copy(k_words[:, :, 0], k_pool[0][:].bitcast(U32).indirect(offsets[:]))
+        for h, width in ((0, PREFIX), (1, T)):
+            nc.vector.tensor_copy(
+                k_words[:, block(h, HALF), 1],
+                k_pool[1][:].bitcast(U32)[:, :width].indirect(offsets[:, block(h, HALF // 16)]),
+            )
+
         for b in range(2):
             scalar_cast(
-                q_grp[:, 4 * b * P : 4 * (b + 1) * P].rearrange("p (c i j) -> p c j i", i=4, j=4),
-                q_raw[:, :, b * P : (b + 1) * P].rearrange("p j (c i) -> p c j i", i=4),
+                q_grp[:, block(b, 4 * P)].rearrange("p (c i j) -> p c j i", i=4, j=4),
+                q_raw[:, :, block(b)].rearrange("p j (c i) -> p c j i", i=4),
             )
         k_cols = shared.tile([P, 2, 16], F32, name="k_cols", offset=0, align_bytes=64)
-        column(ks_bank, k_cols[:, 0, :4])
-        column(kb_bank, k_cols[:, 1, :4])
-        k_codes = keep.tile([P, N], U32, name="k_codes", tag="k1_768", align_bytes=64)
+        scalar_cast(k_cols[:, 0, :4], ks_bank[:, :, LAST])
+        scalar_cast(k_cols[:, 1, :4], kb_bank[:, :, LAST])
+        k_codes = keep.tile([P, N], U32, name="k_codes", tag=f"k1_{PREFIX}", align_bytes=64)
         for h in range(2):
-            cols = slice(h * 256, (h + 1) * 256)
-            nc.vector.quantize_mx(
-                out=k_codes[:, cols].bitcast(FP8X4), scales=k_scale[:, cols], in_=k_grp[:, h * 1024 : (h + 1) * 1024]
-            )
-            cols = slice(h * P, (h + 1) * P)
-            nc.vector.quantize_mx(
-                out=q_codes[:, cols].bitcast(FP8X4), scales=q_scale[:, cols], in_=q_grp[:, h * 512 : (h + 1) * 512]
-            )
+            quantize(k_codes, k_scale, block(h, HALF), k_grp[:, block(h, 4 * HALF)])
+            quantize(q_codes, q_scale, block(h), q_grp[:, block(h, 4 * P)])
 
-        s_t = keep.tile([P, 4, NQ], F32, name="s_t")
+        s_t = keep.tile([P, 4, NQ], F32, name="s_t", tag="s_t", align_bytes=64)
         for b in range(2):
-            q_cols = slice(b * P, (b + 1) * P)
             for h in range(2):
                 bank = psum.tile([P, 2, P], F32, name="qk", tag=f"qk{2 * b + h}")
                 for i in range(2):
-                    sl = slice((2 * h + i) * P, (2 * h + i + 1) * P)
-                    nc.tensor.matmul_mx(
-                        out=bank[:, i, :],
-                        lhsT=k_codes[:, sl].bitcast(FP8X4),
-                        lhsT_scale=k_scale[:, sl],
-                        rhs=q_codes[:, q_cols].bitcast(FP8X4),
-                        rhs_scale=q_scale[:, q_cols],
-                        start=True,
-                        stop=True,
-                    )
+                    product(bank[:, i, :], k_codes, k_scale, block(2 * h + i), q_codes, q_scale, block(b))
                 for i in range(2):
                     c = 2 * h + i
                     nc.scalar.activation(
-                        out=s_t[:, c, q_cols], in_=bank[:, i, :], func=ACT.Identity,
-                        scale=k_cols[:, 0, c : c + 1], bias=k_cols[:, 1, c : c + 1],
+                        out=s_t[:, c, block(b)],
+                        in_=bank[:, i, :],
+                        func=ACT.Identity,
+                        scale=k_cols[:, 0, c : c + 1],
+                        bias=k_cols[:, 1, c : c + 1],
                     )
         vs_col = shared.tile([P, 4], F32, name="vs_col", offset=0, align_bytes=64)
-        column(vs_bank, vs_col[:])
+        scalar_cast(vs_col[:], vs_bank[:, :, LAST])
 
-        v_g = shared.tile([P, 2, N], BF16, name="v_g", offset=2112, align_bytes=64)
+        v_g = [
+            shared.tile([P, N], BF16, name=f"v_g{e}", offset=V_G_AT + V_HALF_BYTES * e, align_bytes=64) for e in range(2)
+        ]
         for e in range(2):
             nc.vector.tensor_copy(
-                v_g[:, e, :].rearrange("p (u s h) -> p s u h", u=2, h=2), v_raw[e][:].indirect(offsets[:])
+                v_g[e][:].rearrange("p (u s h) -> p s u h", u=2, h=2), v_raw[e][:].indirect(offsets[:])
             )
 
         s_banks = [psum.tile([P, N], F32, name=f"s_b{b}", tag=f"s{b}") for b in range(2)]
         for b in range(2):
             for c in range(4):
-                nc.tensor.transpose(s_banks[b][:, c * P : (c + 1) * P], s_t[:, c, b * P : (b + 1) * P], ident[:])
+                nc.tensor.transpose(s_banks[b][:, block(c)], s_t[:, c, block(b)], ident[:])
 
-        v_codes = keep.tile([P, DV], U32, name="v_codes", align_bytes=64)
+        v_codes = keep.tile([P, DV], U32, name="v_codes", tag="s_t", align_bytes=64)
         v_scale = keep.tile([P, DV], U8, name="v_scale", align_bytes=64)
-        v_words = v_g[:].rearrange("p e n -> p (e n)").bitcast(F32)
 
-        def value_half(e, tag, engine_copy):
+        def turn_values(e, tag, engine_copy):
             bank = psum.tile([P, 2, P], F32, name=f"v_t{e}", tag=tag)
             for u in range(2):
-                lo = (2 * e + u) * P
-                nc.tensor.transpose(bank[:, u, :], v_words[:, lo : lo + P], ident[:])
-            v_grp = shared.tile([P, P * 4], BF16, name=f"v_grp{e}", offset=64 + 1024 * e, align_bytes=64)
+                nc.tensor.transpose(bank[:, u, :], v_g[e][:].bitcast(F32)[:, block(u)], ident[:])
+            v_grp = shared.tile(
+                [P, P * 4], BF16, name=f"v_grp{e}", offset=V_GRP_AT + V_HALF_BYTES * e, align_bytes=64
+            )
             engine_copy(v_grp[:].bitcast(F32).rearrange("p (r u) -> p r u", u=2), bank[:].rearrange("p u r -> p r u"))
-            cols = slice(e * P, (e + 1) * P)
-            nc.vector.quantize_mx(out=v_codes[:, cols].bitcast(FP8X4), scales=v_scale[:, cols], in_=v_grp[:])
+            return v_grp
 
-        value_half(0, "acc1", nc.scalar.copy)
-        neg_ms = [keep.tile([P, 1], F32, name=f"neg_m{b}") for b in range(2)]
+        v_grp0 = turn_values(0, "qk2", nc.scalar.copy)
+
+        neg_m = [keep.tile([P, 1], F32, name=f"neg_m{b}") for b in range(2)]
         dealt = [bank[:].rearrange("p (s t) -> p t s", t=4) for bank in s_banks]
         neg_s = keep.tile([P, 4, P], F32, name="neg_s")
         nc.vector.tensor_scalar(
-            out=neg_s[:], in0=dealt[0], scalar1=-1.0, scalar2=None, op0=ALU.mult, op1=ALU.min, accum_out=neg_ms[0][:]
+            out=neg_s[:], in0=dealt[0], scalar1=-1.0, scalar2=None, op0=ALU.mult, op1=ALU.min, accum_out=neg_m[0][:]
         )
-        nc.vector.tensor_reduce(out=neg_ms[1][:], in_=s_banks[1][:], axis=AX.X, op=ALU.max, negate=True)
-        value_half(1, "s0", nc.vector.tensor_copy)
+        nc.vector.tensor_reduce(out=neg_m[1][:], in_=s_banks[1][:], axis=AX.X, op=ALU.max, negate=True)
+        v_grp1 = turn_values(1, "s0", nc.vector.tensor_copy)
+        for e, v_grp in enumerate((v_grp0, v_grp1)):
+            quantize(v_codes, v_scale, block(e), v_grp[:])
 
-        p_tiles = []
+        p_tiles = [keep.tile([P, 4, P], F32, name=f"p{b}") for b in range(2)]
         l_parts = keep.tile([P, 2, 2], F32, name="l_parts")
         for b, (scores, sign) in enumerate(((neg_s[:], -1.0), (dealt[1], 1.0))):
-            p = keep.tile([P, 4, P], F32, name=f"p{b}")
             for h in range(2):
                 nc.scalar.activation(
-                    out=p[:, 2 * h : 2 * h + 2, :],
-                    in_=scores[:, 2 * h : 2 * h + 2, :],
+                    out=p_tiles[b][:, block(h, 2), :],
+                    in_=scores[:, block(h, 2), :],
                     func=ACT.Exp,
                     scale=sign,
-                    bias=neg_ms[b][:],
+                    bias=neg_m[b][:],
                     accum_out=l_parts[:, h, b : b + 1],
                 )
-            p_tiles.append(p)
 
-        w_grps = []
+        w_grp = [keep.tile([P, P * 4], BF16, name=f"w_grp{b}", align_bytes=64) for b in range(2)]
         for b in range(2):
             bank = psum.tile([P, 4, P], F32, name="p_t", tag=f"qk{b}")
             for t in range(4):
                 nc.tensor.transpose(bank[:, t, :], p_tiles[b][:, t, :], ident[:])
-            w_grp = keep.tile([P, P * 4], BF16, name=f"w_grp{b}", align_bytes=64)
             nc.vector.tensor_tensor(
-                out=w_grp[:].rearrange("p (q t) -> p q t", t=4),
+                out=w_grp[b][:].rearrange("p (q t) -> p q t", t=4),
                 in0=bank[:].rearrange("p t q -> p q t"),
                 in1=vs_col[:].unsqueeze(1).to_broadcast([P, P, 4]),
                 op=ALU.mult,
             )
-            w_grps.append(w_grp)
         l_sum = keep.tile([P, 2], F32, name="l_sum")
-        rl = keep.tile([P, 2], F32, name="rl")
+        inv_l = keep.tile([P, 2], F32, name="inv_l")
         nc.vector.tensor_tensor(out=l_sum[:], in0=l_parts[:, 0, :], in1=l_parts[:, 1, :], op=ALU.add)
-        nc.vector.reciprocal(rl[:], l_sum[:])
+        nc.vector.reciprocal(inv_l[:], l_sum[:])
+
         for b in range(2):
             w_codes = keep.tile([P, P], U32, name=f"w_codes{b}", align_bytes=64)
             w_scale = keep.tile([P, P], U8, name=f"w_scale{b}", align_bytes=64)
-            nc.vector.quantize_mx(out=w_codes[:].bitcast(FP8X4), scales=w_scale[:], in_=w_grps[b][:])
+            quantize(w_codes, w_scale, block(0), w_grp[b][:])
             y = keep.tile([P, DV], F32, name=f"y{b}")
-            for lo, hi, tag in ((0, P, f"acc{b}"), (P, DV, f"s{b}")):
-                acc = psum.tile([P, hi - lo], F32, name="acc", tag=tag)
-                nc.tensor.matmul_mx(
-                    out=acc[:],
-                    lhsT=w_codes[:].bitcast(FP8X4),
-                    lhsT_scale=w_scale[:],
-                    rhs=v_codes[:, lo:hi].bitcast(FP8X4),
-                    rhs_scale=v_scale[:, lo:hi],
-                    start=True,
-                    stop=True,
-                )
-                if lo == 0:
-                    nc.scalar.activation(out=y[:, lo:hi], in_=acc[:], func=ACT.Copy, scale=rl[:, b : b + 1])
-                else:
-                    nc.vector.tensor_scalar(out=y[:, lo:hi], in0=acc[:], scalar1=rl[:, b : b + 1], scalar2=None, op0=ALU.mult)
-            nc.sync.dma_start(out[0, b * P : (b + 1) * P, :], y[:])
+            acc = psum.tile([P, P], F32, name="acc_low", tag=f"acc{b}")
+            product(acc[:], w_codes, w_scale, block(0), v_codes, v_scale, block(0))
+            nc.scalar.activation(out=y[:, block(0)], in_=acc[:], func=ACT.Copy, scale=inv_l[:, b : b + 1])
+            acc = psum.tile([P, P], F32, name="acc_high", tag=f"s{b}")
+            product(acc[:], w_codes, w_scale, block(0), v_codes, v_scale, block(1))
+            nc.vector.tensor_scalar(
+                out=y[:, block(1)], in0=acc[:], scalar1=inv_l[:, b : b + 1], scalar2=None, op0=ALU.mult
+            )
+            nc.sync.dma_start(out[0, block(b), :], y[:])

@@ -147,9 +147,7 @@ def tile_attend_x_ks_bias_srt_kernel(tc, qT, kT, vT, ks, vs, kb, offs, out):
             shared.tile([P, N], BF16, name=f"v_g{e}", offset=V_G_AT + V_HALF_BYTES * e, align_bytes=64) for e in range(2)
         ]
         for e in range(2):
-            nc.vector.tensor_copy(
-                v_g[e][:].rearrange("p (u s h) -> p s u h", u=2, h=2), v_raw[e][:].indirect(offsets[:])
-            )
+            nc.vector.tensor_copy(v_g[e][:], v_raw[e][:].indirect(offsets[:]))
 
         s_banks = [psum.tile([P, N], F32, name=f"s_b{b}", tag=f"s{b}") for b in range(2)]
         for b in range(2):
@@ -162,7 +160,7 @@ def tile_attend_x_ks_bias_srt_kernel(tc, qT, kT, vT, ks, vs, kb, offs, out):
         def turn_values(e, tag, engine_copy):
             bank = psum.tile([P, 2, P], F32, name=f"v_t{e}", tag=tag)
             for u in range(2):
-                nc.tensor.transpose(bank[:, u, :], v_g[e][:].bitcast(F32)[:, block(u)], ident[:])
+                nc.tensor.transpose(bank[:, u, :], v_g[e][:].bitcast(F32)[:, u : HALF : 2], ident[:])
             v_grp = shared.tile(
                 [P, P * 4], BF16, name=f"v_grp{e}", offset=V_GRP_AT + V_HALF_BYTES * e, align_bytes=64
             )

@@ -121,25 +121,31 @@ def tile_attend_x_ks_bias_srt_kernel(tc, qT, kT, vT, ks, vs, kb, offs, out):
         scalar_cast(k_cols[:, 0, :4], ks_bank[:, :, LAST])
         scalar_cast(k_cols[:, 1, :4], kb_bank[:, :, LAST])
         k_codes = keep.tile([P, N], U32, name="k_codes", tag=f"k1_{PREFIX}", align_bytes=64)
-        for h in range(2):
-            quantize(k_codes, k_scale, block(h, HALF), k_grp[:, block(h, 4 * HALF)])
-            quantize(q_codes, q_scale, block(h), q_grp[:, block(h, 4 * P)])
+        quantize(k_codes, k_scale, block(0), k_grp[:, block(0, 4 * P)])
+        quantize(q_codes, q_scale, block(0), q_grp[:, block(0, 4 * P)])
+        quantize(k_codes, k_scale, block(1), k_grp[:, block(1, 4 * P)])
+        quantize(k_codes, k_scale, block(1, HALF), k_grp[:, block(1, 4 * HALF)])
+        quantize(q_codes, q_scale, block(1), q_grp[:, block(1, 4 * P)])
 
         s_t = keep.tile([P, 4, NQ], F32, name="s_t", tag="s_t", align_bytes=64)
-        for b in range(2):
-            for h in range(2):
-                bank = psum.tile([P, 2, P], F32, name="qk", tag=f"qk{2 * b + h}")
-                for i in range(2):
-                    product(bank[:, i, :], k_codes, k_scale, block(2 * h + i), q_codes, q_scale, block(b))
-                for i in range(2):
-                    c = 2 * h + i
-                    nc.scalar.activation(
-                        out=s_t[:, c, block(b)],
-                        in_=bank[:, i, :],
-                        func=ACT.Identity,
-                        scale=k_cols[:, 0, c : c + 1],
-                        bias=k_cols[:, 1, c : c + 1],
-                    )
+        for b, tag, chunks in (
+            (0, "acc1", (0,)),
+            (0, "qk0", (1,)),
+            (0, "qk1", (2, 3)),
+            (1, "qk2", (0,)),
+            (1, "qk3", (1, 2, 3)),
+        ):
+            bank = psum.tile([P, len(chunks), P], F32, name="qk", tag=tag)
+            for i, c in enumerate(chunks):
+                product(bank[:, i, :], k_codes, k_scale, block(c), q_codes, q_scale, block(b))
+            for i, c in enumerate(chunks):
+                nc.scalar.activation(
+                    out=s_t[:, c, block(b)],
+                    in_=bank[:, i, :],
+                    func=ACT.Identity,
+                    scale=k_cols[:, 0, c : c + 1],
+                    bias=k_cols[:, 1, c : c + 1],
+                )
         vs_col = shared.tile([P, 4], F32, name="vs_col", offset=0, align_bytes=64)
         scalar_cast(vs_col[:], vs_bank[:, :, LAST])
 
@@ -147,7 +153,9 @@ def tile_attend_x_ks_bias_srt_kernel(tc, qT, kT, vT, ks, vs, kb, offs, out):
             shared.tile([P, N], BF16, name=f"v_g{e}", offset=V_G_AT + V_HALF_BYTES * e, align_bytes=64) for e in range(2)
         ]
         for e in range(2):
-            nc.vector.tensor_copy(v_g[e][:], v_raw[e][:].indirect(offsets[:]))
+            nc.vector.tensor_copy(
+                v_g[e][:].rearrange("p (u s h) -> p s u h", u=2, h=2), v_raw[e][:].indirect(offsets[:])
+            )
 
         s_banks = [psum.tile([P, N], F32, name=f"s_b{b}", tag=f"s{b}") for b in range(2)]
         for b in range(2):
@@ -160,7 +168,7 @@ def tile_attend_x_ks_bias_srt_kernel(tc, qT, kT, vT, ks, vs, kb, offs, out):
         def turn_values(e, tag, engine_copy):
             bank = psum.tile([P, 2, P], F32, name=f"v_t{e}", tag=tag)
             for u in range(2):
-                nc.tensor.transpose(bank[:, u, :], v_g[e][:].bitcast(F32)[:, u : HALF : 2], ident[:])
+                nc.tensor.transpose(bank[:, u, :], v_g[e][:].bitcast(F32)[:, block(u)], ident[:])
             v_grp = shared.tile(
                 [P, P * 4], BF16, name=f"v_grp{e}", offset=V_GRP_AT + V_HALF_BYTES * e, align_bytes=64
             )

@@ -11,6 +11,7 @@ PREFIX = T - HALF
 F32 = mybir.dt.float32
 BF16 = mybir.dt.bfloat16
 U32 = mybir.dt.uint32
+I32 = mybir.dt.int32
 U16 = mybir.dt.uint16
 U8 = mybir.dt.uint8
 FP8X4 = mybir.dt.float8_e4m3fn_x4
@@ -95,21 +96,26 @@ def tile_attend_x_ks_bias_srt_kernel(tc, qT, kT, vT, ks, vs, kb, offs, out):
         kb_bank = turn_table(kb_row, "kb", "s1", block)
         vs_bank = turn_table(vs_row, "vs", "acc0", lambda t: slice(t, N, 4))
 
-        k_grp = keep.tile([P, N * 4], BF16, name="k_grp", align_bytes=64)
+        k_grp = keep.tile([P, N * 4], BF16, name="k_grp", tag=f"k1_{PREFIX}", align_bytes=64)
         q_grp = keep.tile([P, NQ * 4], BF16, name="q_grp", align_bytes=64)
         q_codes = keep.tile([P, NQ], U32, name="q_codes", align_bytes=64)
         q_scale = keep.tile([P, NQ], U8, name="q_scale", align_bytes=64)
         k_scale = keep.tile([P, N], U8, name="k_scale", align_bytes=64)
-        k_words = k_grp[:].bitcast(U32).rearrange("p (i u) -> p i u", u=2)
+        k_words = k_grp[:].bitcast(I32).rearrange("p (i u) -> p i u", u=2)
         for u, lo, hi, raw in pieces:
             scalar_cast(
                 k_pool[u][:, 2 * lo : 2 * hi].rearrange("p (n h) -> p n h", h=2), raw[:].rearrange("p h n -> p n h")
             )
-        nc.vector.tensor_copy(k_words[:, :, 0], k_pool[0][:].bitcast(U32).indirect(offsets[:]))
+        k_g = keep.tile([P, 2, N], U32, name="k_g", align_bytes=64)
+        nc.vector.tensor_copy(k_g[:, 0, :], k_pool[0][:].bitcast(U32).indirect(offsets[:]))
         for h, width in ((0, PREFIX), (1, T)):
             nc.vector.tensor_copy(
-                k_words[:, block(h, HALF), 1],
+                k_g[:, 1, block(h, HALF)],
                 k_pool[1][:].bitcast(U32)[:, :width].indirect(offsets[:, block(h, HALF // 16)]),
+            )
+        for h in range(2):
+            nc.vector.tensor_copy(
+                k_words[:, block(h, HALF), :], k_g[:].bitcast(I32)[:, :, block(h, HALF)].rearrange("p u i -> p i u")
             )
 
         for b in range(2):
@@ -120,7 +126,7 @@ def tile_attend_x_ks_bias_srt_kernel(tc, qT, kT, vT, ks, vs, kb, offs, out):
         k_cols = shared.tile([P, 2, 16], F32, name="k_cols", offset=0, align_bytes=64)
         scalar_cast(k_cols[:, 0, :4], ks_bank[:, :, LAST])
         scalar_cast(k_cols[:, 1, :4], kb_bank[:, :, LAST])
-        k_codes = keep.tile([P, N], U32, name="k_codes", tag=f"k1_{PREFIX}", align_bytes=64)
+        k_codes = keep.tile([P, N], U32, name="k_codes", align_bytes=64)
         quantize(k_codes, k_scale, block(0), k_grp[:, block(0, 4 * P)])
         quantize(q_codes, q_scale, block(0), q_grp[:, block(0, 4 * P)])
         quantize(k_codes, k_scale, block(1), k_grp[:, block(1, 4 * P)])

@@ -19,8 +19,8 @@ ACT = mybir.ActivationFunctionType
 ALU = mybir.AluOpType
 AX = mybir.AxisListType
 
-KEY_CUTS = ((0, 256, 640, T), (0, 384, PREFIX, T))
-GPSIMD_CLEARS = 384
+KEY_LOADS = ((0, 0, 256), (0, 256, T), (1, 0, PREFIX), (1, PREFIX, T))
+KEY_SPLITS = (256, 768, 384, T)
 V_GRP_AT = 64
 V_HALF_BYTES = 1024
 V_G_AT = V_GRP_AT + 2 * V_HALF_BYTES
@@ -64,20 +64,16 @@ def tile_attend_x_ks_bias_srt_kernel(tc, qT, kT, vT, ks, vs, kb, offs, out):
         nc.sync.dma_start(offsets[:], offs)
         for row, table in ((ks_row, ks), (kb_row, kb), (vs_row, vs)):
             nc.scalar.dma_start(row[LAST:, :], table[LAST:, :])
-        for row in (ks_row, kb_row):
-            nc.gpsimd.memset(row[:LAST, :GPSIMD_CLEARS], 0.0)
-            nc.vector.memset(row[:LAST, GPSIMD_CLEARS:], 0.0)
+        for row in (ks_row, kb_row, vs_row):
+            nc.vector.memset(row[:LAST, :], 0.0)
         make_identity(nc, ident[:])
-        nc.gpsimd.memset(vs_row[:LAST, :], 0.0)
 
         k_planes = kT.rearrange("(p j) n -> p j n", j=4)
-        k_pool = [keep.tile([P, T * 2], BF16, name=f"k_pool{u}", align_bytes=64) for u in range(2)]
-        pieces = []
-        for u, cuts in enumerate(KEY_CUTS):
-            for lo, hi in zip(cuts, cuts[1:]):
-                raw = keep.tile([P, 2, hi - lo], F32, name=f"k{u}_{lo}", tag=f"k{u}_{lo}", align_bytes=64)
-                nc.sync.dma_start(raw[:], k_planes[:, 2 * u : 2 * u + 2, lo:hi])
-                pieces.append((u, lo, hi, raw))
+        raws = []
+        for u, lo, hi in KEY_LOADS:
+            raw = keep.tile([P, 2, hi - lo], F32, name=f"k{u}_{lo}", tag=f"k{u}_{lo}", align_bytes=64)
+            nc.sync.dma_start(raw[:], k_planes[:, 2 * u : 2 * u + 2, lo:hi])
+            raws.append(raw)
         q_raw = shared.tile([P, 4, NQ], F32, name="q_raw", offset=0, align_bytes=64)
         nc.sync.dma_start(q_raw[:], qT[0].rearrange("(p j) n -> p j n", j=4))
         v_raw = [keep.tile([P, T], F32, name=f"v_raw{e}") for e in range(2)]
@@ -102,10 +98,17 @@ def tile_attend_x_ks_bias_srt_kernel(tc, qT, kT, vT, ks, vs, kb, offs, out):
         q_scale = keep.tile([P, NQ], U8, name="q_scale", align_bytes=64)
         k_scale = keep.tile([P, N], U8, name="k_scale", align_bytes=64)
         k_words = k_grp[:].bitcast(I32).rearrange("p (i u) -> p i u", u=2)
-        for u, lo, hi, raw in pieces:
-            scalar_cast(
-                k_pool[u][:, 2 * lo : 2 * hi].rearrange("p (n h) -> p n h", h=2), raw[:].rearrange("p h n -> p n h")
-            )
+        k_pool = [
+            keep.tile([P, T * 2], BF16, name="k_pool0", align_bytes=64),
+            keep.tile([P, T * 2], BF16, name="k_pool1", tag="k0_256", align_bytes=64),
+        ]
+        for (u, lo, hi), raw, split in zip(KEY_LOADS, raws, KEY_SPLITS):
+            for cast, first, last in ((scalar_cast, lo, split), (nc.vector.tensor_copy, split, hi)):
+                if first < last:
+                    cast(
+                        k_pool[u][:, 2 * first : 2 * last].rearrange("p (n h) -> p n h", h=2),
+                        raw[:, :, first - lo : last - lo].rearrange("p h n -> p n h"),
+                    )
         k_g = keep.tile([P, 2, N], U32, name="k_g", align_bytes=64)
         nc.vector.tensor_copy(k_g[:, 0, :], k_pool[0][:].bitcast(U32).indirect(offsets[:]))
         for h, width in ((0, PREFIX), (1, T)):

@@ -7,11 +7,9 @@ P = 128
 LAST = P - 1
 D, T, N, NQ, DV = 512, 1024, 512, 256, 256
 HALF = N // 2
-PREFIX = T - HALF
 F32 = mybir.dt.float32
 BF16 = mybir.dt.bfloat16
 U32 = mybir.dt.uint32
-I32 = mybir.dt.int32
 U16 = mybir.dt.uint16
 U8 = mybir.dt.uint8
 FP8X4 = mybir.dt.float8_e4m3fn_x4
@@ -19,11 +17,10 @@ ACT = mybir.ActivationFunctionType
 ALU = mybir.AluOpType
 AX = mybir.AxisListType
 
-KEY_LOADS = ((0, 0, 256), (0, 256, T), (1, 0, PREFIX), (1, PREFIX, T))
-KEY_SPLITS = (256, 768, 384, T)
-V_GRP_AT = 64
 V_HALF_BYTES = 1024
-V_G_AT = V_GRP_AT + 2 * V_HALF_BYTES
+V_G_AT = 0
+K_COLS_AT = 4096
+V_GRP_AT = K_COLS_AT + 64
 
 FLOPS = 2 * NQ * N * (D + DV)
 BYTES = 4 * (D * NQ + (D + DV) * N + 3 * N + NQ * DV) + 2 * N
@@ -66,14 +63,15 @@ def tile_attend_x_ks_bias_srt_kernel(tc, qT, kT, vT, ks, vs, kb, offs, out):
             nc.scalar.dma_start(row[LAST:, :], table[LAST:, :])
         for row in (ks_row, kb_row, vs_row):
             nc.vector.memset(row[:LAST, :], 0.0)
+        warm = keep.tile([P, 2], F32, name="warm")
+        nc.gpsimd.memset(warm[:, :1], 0.0)
+        nc.scalar.activation(out=warm[:, 1:], in_=warm[:, :1], func=ACT.Exp)
         make_identity(nc, ident[:])
 
         k_planes = kT.rearrange("(p j) n -> p j n", j=4)
-        raws = []
-        for u, lo, hi in KEY_LOADS:
-            raw = keep.tile([P, 2, hi - lo], F32, name=f"k{u}_{lo}", tag=f"k{u}_{lo}", align_bytes=64)
-            nc.sync.dma_start(raw[:], k_planes[:, 2 * u : 2 * u + 2, lo:hi])
-            raws.append(raw)
+        k_raw = [keep.tile([P, T], F32, name=f"k_raw{j}") for j in range(4)]
+        for j in range(4):
+            nc.sync.dma_start(k_raw[j][:], k_planes[:, j, :])
         q_raw = shared.tile([P, 4, NQ], F32, name="q_raw", offset=0, align_bytes=64)
         nc.sync.dma_start(q_raw[:], qT[0].rearrange("(p j) n -> p j n", j=4))
         v_raw = [keep.tile([P, T], F32, name=f"v_raw{e}") for e in range(2)]
@@ -82,7 +80,7 @@ def tile_attend_x_ks_bias_srt_kernel(tc, qT, kT, vT, ks, vs, kb, offs, out):
 
         def turn_table(row, name, tag, slots):
             gathered = keep.tile([P, N], F32, name=name + "_g")
-            nc.vector.tensor_copy(gathered[:], row[:].indirect(offsets[:]))
+            scalar_cast(gathered[:], row[:].indirect(offsets[:]))
             bank = psum.tile([P, 4, P], F32, name=name + "_t", tag=tag)
             for c in range(4):
                 nc.tensor.transpose(bank[:, c, :], gathered[:, slots(c)], ident[:])
@@ -92,47 +90,42 @@ def tile_attend_x_ks_bias_srt_kernel(tc, qT, kT, vT, ks, vs, kb, offs, out):
         kb_bank = turn_table(kb_row, "kb", "s1", block)
         vs_bank = turn_table(vs_row, "vs", "acc0", lambda t: slice(t, N, 4))
 
-        k_grp = keep.tile([P, N * 4], BF16, name="k_grp", tag=f"k1_{PREFIX}", align_bytes=64)
+        k_cols = shared.tile([P, 2, 16], F32, name="k_cols", offset=K_COLS_AT, align_bytes=64)
+        scalar_cast(k_cols[:, 0, :4], ks_bank[:, :, LAST])
+        scalar_cast(k_cols[:, 1, :4], kb_bank[:, :, LAST])
+        vs_col = keep.tile([P, 4], F32, name="vs_col")
+        scalar_cast(vs_col[:], vs_bank[:, :, LAST])
+
+        k_g = keep.tile([P, 4, N], BF16, name="k_g", align_bytes=64)
+        k_grp = keep.tile([P, N * 4], BF16, name="k_grp", align_bytes=64)
         q_grp = keep.tile([P, NQ * 4], BF16, name="q_grp", align_bytes=64)
         q_codes = keep.tile([P, NQ], U32, name="q_codes", align_bytes=64)
         q_scale = keep.tile([P, NQ], U8, name="q_scale", align_bytes=64)
+        k_codes = keep.tile([P, N], U32, name="k_codes", align_bytes=64)
         k_scale = keep.tile([P, N], U8, name="k_scale", align_bytes=64)
-        k_words = k_grp[:].bitcast(I32).rearrange("p (i u) -> p i u", u=2)
-        k_pool = [
-            keep.tile([P, T * 2], BF16, name="k_pool0", align_bytes=64),
-            keep.tile([P, T * 2], BF16, name="k_pool1", tag="k0_256", align_bytes=64),
-        ]
-        for (u, lo, hi), raw, split in zip(KEY_LOADS, raws, KEY_SPLITS):
-            for cast, first, last in ((scalar_cast, lo, split), (nc.vector.tensor_copy, split, hi)):
-                if first < last:
-                    cast(
-                        k_pool[u][:, 2 * first : 2 * last].rearrange("p (n h) -> p n h", h=2),
-                        raw[:, :, first - lo : last - lo].rearrange("p h n -> p n h"),
-                    )
-        k_g = keep.tile([P, 2, N], U32, name="k_g", align_bytes=64)
-        nc.vector.tensor_copy(k_g[:, 0, :], k_pool[0][:].bitcast(U32).indirect(offsets[:]))
-        for h, width in ((0, PREFIX), (1, T)):
-            nc.vector.tensor_copy(
-                k_g[:, 1, block(h, HALF)],
-                k_pool[1][:].bitcast(U32)[:, :width].indirect(offsets[:, block(h, HALF // 16)]),
-            )
-        for h in range(2):
-            nc.vector.tensor_copy(
-                k_words[:, block(h, HALF), :], k_g[:].bitcast(I32)[:, :, block(h, HALF)].rearrange("p u i -> p i u")
+        for j in range(3):
+            nc.vector.tensor_copy(k_g[:, j, :], k_raw[j][:].indirect(offsets[:]))
+        for h, gather in enumerate((nc.vector.tensor_copy, scalar_cast)):
+            gather(k_g[:, 3, block(h, HALF)], k_raw[3][:].indirect(offsets[:, block(h, HALF // 16)]))
+
+        def weave(slots, engine_copy=nc.vector.tensor_copy):
+            engine_copy(
+                k_grp[:].rearrange("p (n j) -> p n j", j=4)[:, slots, :].rearrange("p (c i) j -> p c j i", i=4),
+                k_g[:, :, slots].rearrange("p j (c i) -> p c j i", i=4),
             )
 
+        weave(block(3), nc.scalar.copy)
         for b in range(2):
             scalar_cast(
                 q_grp[:, block(b, 4 * P)].rearrange("p (c i j) -> p c j i", i=4, j=4),
                 q_raw[:, :, block(b)].rearrange("p j (c i) -> p c j i", i=4),
             )
-        k_cols = shared.tile([P, 2, 16], F32, name="k_cols", offset=0, align_bytes=64)
-        scalar_cast(k_cols[:, 0, :4], ks_bank[:, :, LAST])
-        scalar_cast(k_cols[:, 1, :4], kb_bank[:, :, LAST])
-        k_codes = keep.tile([P, N], U32, name="k_codes", align_bytes=64)
+        weave(block(0))
+        weave(block(1))
         quantize(k_codes, k_scale, block(0), k_grp[:, block(0, 4 * P)])
-        quantize(q_codes, q_scale, block(0), q_grp[:, block(0, 4 * P)])
+        weave(block(2))
         quantize(k_codes, k_scale, block(1), k_grp[:, block(1, 4 * P)])
+        quantize(q_codes, q_scale, block(0), q_grp[:, block(0, 4 * P)])
         quantize(k_codes, k_scale, block(1, HALF), k_grp[:, block(1, 4 * HALF)])
         quantize(q_codes, q_scale, block(1), q_grp[:, block(1, 4 * P)])
 
@@ -155,8 +148,6 @@ def tile_attend_x_ks_bias_srt_kernel(tc, qT, kT, vT, ks, vs, kb, offs, out):
                     scale=k_cols[:, 0, c : c + 1],
                     bias=k_cols[:, 1, c : c + 1],
                 )
-        vs_col = shared.tile([P, 4], F32, name="vs_col", offset=0, align_bytes=64)
-        scalar_cast(vs_col[:], vs_bank[:, :, LAST])
 
         v_g = [
             shared.tile([P, N], BF16, name=f"v_g{e}", offset=V_G_AT + V_HALF_BYTES * e, align_bytes=64) for e in range(2)

@@ -7,6 +7,7 @@ P = 128
 LAST = P - 1
 D, T, N, NQ, DV = 512, 1024, 512, 256, 256
 HALF = N // 2
+PREFIX = T - HALF
 F32 = mybir.dt.float32
 BF16 = mybir.dt.bfloat16
 U32 = mybir.dt.uint32
@@ -19,8 +20,8 @@ AX = mybir.AxisListType
 
 V_HALF_BYTES = 1024
 V_G_AT = 0
-K_COLS_AT = 4096
-V_GRP_AT = K_COLS_AT + 64
+NEG_M_AT = 4096
+V_GRP_AT = NEG_M_AT
 
 FLOPS = 2 * NQ * N * (D + DV)
 BYTES = 4 * (D * NQ + (D + DV) * N + 3 * N + NQ * DV) + 2 * N
@@ -61,42 +62,43 @@ def tile_attend_x_ks_bias_srt_kernel(tc, qT, kT, vT, ks, vs, kb, offs, out):
         nc.sync.dma_start(offsets[:], offs)
         for row, table in ((ks_row, ks), (kb_row, kb), (vs_row, vs)):
             nc.scalar.dma_start(row[LAST:, :], table[LAST:, :])
-        for row in (ks_row, kb_row, vs_row):
+        for row in (ks_row, kb_row):
             nc.vector.memset(row[:LAST, :], 0.0)
-        warm = keep.tile([P, 2], F32, name="warm")
-        nc.gpsimd.memset(warm[:, :1], 0.0)
-        nc.scalar.activation(out=warm[:, 1:], in_=warm[:, :1], func=ACT.Exp)
+        nc.gpsimd.memset(vs_row[:LAST, :], 0.0)
         make_identity(nc, ident[:])
 
         k_planes = kT.rearrange("(p j) n -> p j n", j=4)
         k_raw = [keep.tile([P, T], F32, name=f"k_raw{j}") for j in range(4)]
-        for j in range(4):
+        for j in range(3):
             nc.sync.dma_start(k_raw[j][:], k_planes[:, j, :])
+        for tokens in (slice(0, PREFIX), slice(PREFIX, T)):
+            nc.sync.dma_start(k_raw[3][:, tokens], k_planes[:, 3, tokens])
         q_raw = shared.tile([P, 4, NQ], F32, name="q_raw", offset=0, align_bytes=64)
         nc.sync.dma_start(q_raw[:], qT[0].rearrange("(p j) n -> p j n", j=4))
         v_raw = [keep.tile([P, T], F32, name=f"v_raw{e}") for e in range(2)]
         for e in range(2):
             nc.sync.dma_start(v_raw[e][:], vT[block(e), :])
 
-        def turn_table(row, name, tag, slots):
+        def turn_table(row, name, tag, slots, gather):
             gathered = keep.tile([P, N], F32, name=name + "_g")
-            scalar_cast(gathered[:], row[:].indirect(offsets[:]))
+            gather(gathered[:], row[:].indirect(offsets[:]))
             bank = psum.tile([P, 4, P], F32, name=name + "_t", tag=tag)
             for c in range(4):
                 nc.tensor.transpose(bank[:, c, :], gathered[:, slots(c)], ident[:])
             return bank
 
-        ks_bank = turn_table(ks_row, "ks", "s0", block)
-        kb_bank = turn_table(kb_row, "kb", "s1", block)
-        vs_bank = turn_table(vs_row, "vs", "acc0", lambda t: slice(t, N, 4))
+        ks_bank = turn_table(ks_row, "ks", "s0", block, nc.vector.tensor_copy)
+        kb_bank = turn_table(kb_row, "kb", "s1", block, scalar_cast)
+        vs_bank = turn_table(vs_row, "vs", "acc0", lambda t: slice(t, N, 4), scalar_cast)
 
-        k_cols = shared.tile([P, 2, 16], F32, name="k_cols", offset=K_COLS_AT, align_bytes=64)
+        v_late = keep.tile([P, N], BF16, name="v_late", align_bytes=64)
+        k_cols = v_late[:, :64].bitcast(F32).rearrange("p (a c) -> p a c", a=2)
         scalar_cast(k_cols[:, 0, :4], ks_bank[:, :, LAST])
         scalar_cast(k_cols[:, 1, :4], kb_bank[:, :, LAST])
         vs_col = keep.tile([P, 4], F32, name="vs_col")
         scalar_cast(vs_col[:], vs_bank[:, :, LAST])
 
-        k_g = keep.tile([P, 4, N], BF16, name="k_g", align_bytes=64)
+        k_g = keep.tile([P, 4, 4, P], BF16, name="k_g", align_bytes=64)
         k_grp = keep.tile([P, N * 4], BF16, name="k_grp", align_bytes=64)
         q_grp = keep.tile([P, NQ * 4], BF16, name="q_grp", align_bytes=64)
         q_codes = keep.tile([P, NQ], U32, name="q_codes", align_bytes=64)
@@ -104,30 +106,29 @@ def tile_attend_x_ks_bias_srt_kernel(tc, qT, kT, vT, ks, vs, kb, offs, out):
         k_codes = keep.tile([P, N], U32, name="k_codes", align_bytes=64)
         k_scale = keep.tile([P, N], U8, name="k_scale", align_bytes=64)
         for j in range(3):
-            nc.vector.tensor_copy(k_g[:, j, :], k_raw[j][:].indirect(offsets[:]))
-        for h, gather in enumerate((nc.vector.tensor_copy, scalar_cast)):
-            gather(k_g[:, 3, block(h, HALF)], k_raw[3][:].indirect(offsets[:, block(h, HALF // 16)]))
+            nc.vector.tensor_copy(k_g[:, :, j, :], k_raw[j][:].indirect(offsets[:]))
+        nc.vector.tensor_copy(k_g[:, :2, 3, :], k_raw[3][:, :PREFIX].indirect(offsets[:, : HALF // 16]))
+        for c in (3, 2):
+            scalar_cast(k_g[:, c, 3, :], k_raw[3][:].indirect(offsets[:, block(c, P // 16)]))
 
-        def weave(slots, engine_copy=nc.vector.tensor_copy):
+        def weave(c, engine_copy):
             engine_copy(
-                k_grp[:].rearrange("p (n j) -> p n j", j=4)[:, slots, :].rearrange("p (c i) j -> p c j i", i=4),
-                k_g[:, :, slots].rearrange("p j (c i) -> p c j i", i=4),
+                k_grp[:, block(c, 4 * P)].rearrange("p (g i j) -> p g j i", i=4, j=4),
+                k_g[:, c, :, :].rearrange("p j (g i) -> p g j i", i=4),
             )
 
-        weave(block(3), nc.scalar.copy)
+        weave(3, nc.scalar.copy)
         for b in range(2):
             scalar_cast(
                 q_grp[:, block(b, 4 * P)].rearrange("p (c i j) -> p c j i", i=4, j=4),
                 q_raw[:, :, block(b)].rearrange("p j (c i) -> p c j i", i=4),
             )
-        weave(block(0))
-        weave(block(1))
-        quantize(k_codes, k_scale, block(0), k_grp[:, block(0, 4 * P)])
-        weave(block(2))
-        quantize(k_codes, k_scale, block(1), k_grp[:, block(1, 4 * P)])
-        quantize(q_codes, q_scale, block(0), q_grp[:, block(0, 4 * P)])
-        quantize(k_codes, k_scale, block(1, HALF), k_grp[:, block(1, 4 * HALF)])
-        quantize(q_codes, q_scale, block(1), q_grp[:, block(1, 4 * P)])
+        for c in range(3):
+            weave(c, nc.vector.tensor_copy)
+        for h in range(2):
+            quantize(k_codes, k_scale, block(h, HALF), k_grp[:, block(h, 4 * HALF)])
+        for b in range(2):
+            quantize(q_codes, q_scale, block(b), q_grp[:, block(b, 4 * P)])
 
         s_t = keep.tile([P, 4, NQ], F32, name="s_t", tag="s_t", align_bytes=64)
         for b, tag, chunks in (
@@ -149,13 +150,11 @@ def tile_attend_x_ks_bias_srt_kernel(tc, qT, kT, vT, ks, vs, kb, offs, out):
                     bias=k_cols[:, 1, c : c + 1],
                 )
 
-        v_g = [
-            shared.tile([P, N], BF16, name=f"v_g{e}", offset=V_G_AT + V_HALF_BYTES * e, align_bytes=64) for e in range(2)
-        ]
-        for e in range(2):
-            nc.vector.tensor_copy(
-                v_g[e][:].rearrange("p (u s h) -> p s u h", u=2, h=2), v_raw[e][:].indirect(offsets[:])
-            )
+        v_g = [shared.tile([P, N], BF16, name="v_early", offset=V_G_AT, align_bytes=64), v_late]
+        nc.vector.tensor_copy(v_g[0][:].rearrange("p (u s h) -> p s u h", u=2, h=2), v_raw[0][:].indirect(offsets[:]))
+        for h, gather in enumerate((scalar_cast, nc.vector.tensor_copy)):
+            gather(v_late[:, block(h, HALF)], v_raw[1][:].indirect(offsets[:, block(h, HALF // 16)]))
+        v_words = (block, lambda u: slice(u, 2 * P, 2))
 
         s_banks = [psum.tile([P, N], F32, name=f"s_b{b}", tag=f"s{b}") for b in range(2)]
         for b in range(2):
@@ -168,16 +167,15 @@ def tile_attend_x_ks_bias_srt_kernel(tc, qT, kT, vT, ks, vs, kb, offs, out):
         def turn_values(e, tag, engine_copy):
             bank = psum.tile([P, 2, P], F32, name=f"v_t{e}", tag=tag)
             for u in range(2):
-                nc.tensor.transpose(bank[:, u, :], v_g[e][:].bitcast(F32)[:, block(u)], ident[:])
+                nc.tensor.transpose(bank[:, u, :], v_g[e][:].bitcast(F32)[:, v_words[e](u)], ident[:])
             v_grp = shared.tile(
                 [P, P * 4], BF16, name=f"v_grp{e}", offset=V_GRP_AT + V_HALF_BYTES * e, align_bytes=64
             )
             engine_copy(v_grp[:].bitcast(F32).rearrange("p (r u) -> p r u", u=2), bank[:].rearrange("p u r -> p r u"))
             return v_grp
 
-        v_grp0 = turn_values(0, "qk2", nc.scalar.copy)
 
-        neg_m = [keep.tile([P, 1], F32, name=f"neg_m{b}") for b in range(2)]
+        neg_m = [keep.tile([P, 1], F32, name="neg_m0"), shared.tile([P, 1], F32, name="neg_m1", offset=NEG_M_AT)]
         dealt = [bank[:].rearrange("p (s t) -> p t s", t=4) for bank in s_banks]
         neg_s = keep.tile([P, 4, P], F32, name="neg_s")
         nc.vector.tensor_scalar(
@@ -185,8 +183,7 @@ def tile_attend_x_ks_bias_srt_kernel(tc, qT, kT, vT, ks, vs, kb, offs, out):
         )
         nc.vector.tensor_reduce(out=neg_m[1][:], in_=s_banks[1][:], axis=AX.X, op=ALU.max, negate=True)
         v_grp1 = turn_values(1, "s0", nc.vector.tensor_copy)
-        for e, v_grp in enumerate((v_grp0, v_grp1)):
-            quantize(v_codes, v_scale, block(e), v_grp[:])
+        quantize(v_codes, v_scale, block(1), v_grp1[:])
 
         p_tiles = [keep.tile([P, 4, P], F32, name=f"p{b}") for b in range(2)]
         l_parts = keep.tile([P, 2, 2], F32, name="l_parts")
@@ -201,6 +198,7 @@ def tile_attend_x_ks_bias_srt_kernel(tc, qT, kT, vT, ks, vs, kb, offs, out):
                     accum_out=l_parts[:, h, b : b + 1],
                 )
 
+        v_grp0 = turn_values(0, "qk2", nc.scalar.copy)
         w_grp = [keep.tile([P, P * 4], BF16, name=f"w_grp{b}", align_bytes=64) for b in range(2)]
         for b in range(2):
             bank = psum.tile([P, 4, P], F32, name="p_t", tag=f"qk{b}")
@@ -212,6 +210,7 @@ def tile_attend_x_ks_bias_srt_kernel(tc, qT, kT, vT, ks, vs, kb, offs, out):
                 in1=vs_col[:].unsqueeze(1).to_broadcast([P, P, 4]),
                 op=ALU.mult,
             )
+        quantize(v_codes, v_scale, block(0), v_grp0[:])
         l_sum = keep.tile([P, 2], F32, name="l_sum")
         inv_l = keep.tile([P, 2], F32, name="inv_l")
         nc.vector.tensor_tensor(out=l_sum[:], in0=l_parts[:, 0, :], in1=l_parts[:, 1, :], op=ALU.add)

@@ -18,10 +18,9 @@ ACT = mybir.ActivationFunctionType
 ALU = mybir.AluOpType
 AX = mybir.AxisListType
 
-V_HALF_BYTES = 1024
 V_G_AT = 0
-NEG_M_AT = 4096
-V_GRP_AT = NEG_M_AT
+P_LAST_AT = 4096
+NEG_M_AT = 6144
 
 FLOPS = 2 * NQ * N * (D + DV)
 BYTES = 4 * (D * NQ + (D + DV) * N + 3 * N + NQ * DV) + 2 * N
@@ -91,8 +90,7 @@ def tile_attend_x_ks_bias_srt_kernel(tc, qT, kT, vT, ks, vs, kb, offs, out):
         kb_bank = turn_table(kb_row, "kb", "s1", block, scalar_cast)
         vs_bank = turn_table(vs_row, "vs", "acc0", lambda t: slice(t, N, 4), scalar_cast)
 
-        v_late = keep.tile([P, N], BF16, name="v_late", align_bytes=64)
-        k_cols = v_late[:, :64].bitcast(F32).rearrange("p (a c) -> p a c", a=2)
+        k_cols = keep.tile([P, 2, 4], F32, name="k_cols")
         scalar_cast(k_cols[:, 0, :4], ks_bank[:, :, LAST])
         scalar_cast(k_cols[:, 1, :4], kb_bank[:, :, LAST])
         vs_col = keep.tile([P, 4], F32, name="vs_col")
@@ -100,7 +98,7 @@ def tile_attend_x_ks_bias_srt_kernel(tc, qT, kT, vT, ks, vs, kb, offs, out):
 
         k_g = keep.tile([P, 4, 4, P], BF16, name="k_g", align_bytes=64)
         k_grp = keep.tile([P, N * 4], BF16, name="k_grp", align_bytes=64)
-        q_grp = keep.tile([P, NQ * 4], BF16, name="q_grp", align_bytes=64)
+        q_grp = [keep.tile([P, 4 * P], BF16, name=f"q_grp{b}", tag=f"q_grp{b}", align_bytes=64)[:] for b in range(2)]
         q_codes = keep.tile([P, NQ], U32, name="q_codes", align_bytes=64)
         q_scale = keep.tile([P, NQ], U8, name="q_scale", align_bytes=64)
         k_codes = keep.tile([P, N], U32, name="k_codes", align_bytes=64)
@@ -120,7 +118,7 @@ def tile_attend_x_ks_bias_srt_kernel(tc, qT, kT, vT, ks, vs, kb, offs, out):
         weave(3, nc.scalar.copy)
         for b in range(2):
             scalar_cast(
-                q_grp[:, block(b, 4 * P)].rearrange("p (c i j) -> p c j i", i=4, j=4),
+                q_grp[b].rearrange("p (c i j) -> p c j i", i=4, j=4),
                 q_raw[:, :, block(b)].rearrange("p j (c i) -> p c j i", i=4),
             )
         for c in range(3):
@@ -128,15 +126,15 @@ def tile_attend_x_ks_bias_srt_kernel(tc, qT, kT, vT, ks, vs, kb, offs, out):
         for h in range(2):
             quantize(k_codes, k_scale, block(h, HALF), k_grp[:, block(h, 4 * HALF)])
         for b in range(2):
-            quantize(q_codes, q_scale, block(b), q_grp[:, block(b, 4 * P)])
+            quantize(q_codes, q_scale, block(b), q_grp[b])
 
-        s_t = keep.tile([P, 4, NQ], F32, name="s_t", tag="s_t", align_bytes=64)
+        s_t = keep.tile([P, 4, NQ], F32, name="s_t", align_bytes=64)
         for b, tag, chunks in (
-            (0, "acc1", (0,)),
-            (0, "qk0", (1,)),
-            (0, "qk1", (2, 3)),
-            (1, "qk2", (0,)),
-            (1, "qk3", (1, 2, 3)),
+            (0, "qk0", (0,)),
+            (0, "qk1", (1,)),
+            (0, "qk2", (2, 3)),
+            (1, "qk3", (0, 1)),
+            (1, "qk4", (2, 3)),
         ):
             bank = psum.tile([P, len(chunks), P], F32, name="qk", tag=tag)
             for i, c in enumerate(chunks):
@@ -150,55 +148,60 @@ def tile_attend_x_ks_bias_srt_kernel(tc, qT, kT, vT, ks, vs, kb, offs, out):
                     bias=k_cols[:, 1, c : c + 1],
                 )
 
-        v_g = [shared.tile([P, N], BF16, name="v_early", offset=V_G_AT, align_bytes=64), v_late]
-        nc.vector.tensor_copy(v_g[0][:].rearrange("p (u s h) -> p s u h", u=2, h=2), v_raw[0][:].indirect(offsets[:]))
-        for h, gather in enumerate((scalar_cast, nc.vector.tensor_copy)):
-            gather(v_late[:, block(h, HALF)], v_raw[1][:].indirect(offsets[:, block(h, HALF // 16)]))
-        v_words = (block, lambda u: slice(u, 2 * P, 2))
+        v_early = shared.tile([P, N], BF16, name="v_early", offset=V_G_AT, align_bytes=64)
+        v_late = keep.tile([P, N], BF16, name="v_late", tag="q_grp1", align_bytes=64)
+        v_g = [v_early[:], v_late[:]]
+        for e in range(2):
+            nc.vector.tensor_copy(v_g[e].rearrange("p (u s h) -> p s u h", u=2, h=2), v_raw[e][:].indirect(offsets[:]))
 
         s_banks = [psum.tile([P, N], F32, name=f"s_b{b}", tag=f"s{b}") for b in range(2)]
         for b in range(2):
             for c in range(4):
                 nc.tensor.transpose(s_banks[b][:, block(c)], s_t[:, c, block(b)], ident[:])
 
-        v_codes = keep.tile([P, DV], U32, name="v_codes", tag="s_t", align_bytes=64)
-        v_scale = keep.tile([P, DV], U8, name="v_scale", align_bytes=64)
-
-        def turn_values(e, tag, engine_copy):
-            bank = psum.tile([P, 2, P], F32, name=f"v_t{e}", tag=tag)
-            for u in range(2):
-                nc.tensor.transpose(bank[:, u, :], v_g[e][:].bitcast(F32)[:, v_words[e](u)], ident[:])
-            v_grp = shared.tile(
-                [P, P * 4], BF16, name=f"v_grp{e}", offset=V_GRP_AT + V_HALF_BYTES * e, align_bytes=64
-            )
-            engine_copy(v_grp[:].bitcast(F32).rearrange("p (r u) -> p r u", u=2), bank[:].rearrange("p u r -> p r u"))
-            return v_grp
-
-
         neg_m = [keep.tile([P, 1], F32, name="neg_m0"), shared.tile([P, 1], F32, name="neg_m1", offset=NEG_M_AT)]
-        dealt = [bank[:].rearrange("p (s t) -> p t s", t=4) for bank in s_banks]
-        neg_s = keep.tile([P, 4, P], F32, name="neg_s")
-        nc.vector.tensor_scalar(
-            out=neg_s[:], in0=dealt[0], scalar1=-1.0, scalar2=None, op0=ALU.mult, op1=ALU.min, accum_out=neg_m[0][:]
-        )
-        nc.vector.tensor_reduce(out=neg_m[1][:], in_=s_banks[1][:], axis=AX.X, op=ALU.max, negate=True)
-        v_grp1 = turn_values(1, "s0", nc.vector.tensor_copy)
-        quantize(v_codes, v_scale, block(1), v_grp1[:])
+        for b in range(2):
+            nc.vector.tensor_reduce(out=neg_m[b][:], in_=s_banks[b][:], axis=AX.X, op=ALU.max, negate=True)
 
-        p_tiles = [keep.tile([P, 4, P], F32, name=f"p{b}") for b in range(2)]
+        v_banks = [psum.tile([P, 2, P], F32, name=f"v_t{e}", tag=f"qk{4 - e}") for e in range(2)]
+        for e in range(2):
+            for u in range(2):
+                nc.tensor.transpose(v_banks[e][:, u, :], v_g[e].bitcast(F32)[:, block(u)], ident[:])
+        v_grp = [
+            keep.tile([P, P * 4], BF16, name="v_grp0", align_bytes=64),
+            shared.tile([P, P * 4], BF16, name="v_grp1", offset=NEG_M_AT, align_bytes=64),
+        ]
+        v_codes = [
+            keep.tile([P, P], U32, name="v_codes0", align_bytes=64),
+            shared.tile([P, P], U32, name="v_codes1", offset=P_LAST_AT + 512, align_bytes=64),
+        ]
+        v_scale = [keep.tile([P, P], U8, name=f"v_scale{e}", align_bytes=64) for e in range(2)]
+
+        def copy_values(e, engine_copy):
+            engine_copy(
+                v_grp[e][:].bitcast(F32).rearrange("p (r u) -> p r u", u=2), v_banks[e][:].rearrange("p u r -> p r u")
+            )
+
+        copy_values(0, nc.vector.tensor_copy)
+        quantize(v_codes[0], v_scale[0], block(0), v_grp[0][:])
+
+        p_tiles = [
+            keep.tile([P, 4, P], F32, name="p0"),
+            shared.tile([P, 4, P], F32, name="p1", offset=P_LAST_AT, align_bytes=64),
+        ]
         l_parts = keep.tile([P, 2, 2], F32, name="l_parts")
-        for b, (scores, sign) in enumerate(((neg_s[:], -1.0), (dealt[1], 1.0))):
+        for b in range(2):
+            dealt = s_banks[b][:].rearrange("p (s t) -> p t s", t=4)
             for h in range(2):
                 nc.scalar.activation(
                     out=p_tiles[b][:, block(h, 2), :],
-                    in_=scores[:, block(h, 2), :],
+                    in_=dealt[:, block(h, 2), :],
                     func=ACT.Exp,
-                    scale=sign,
                     bias=neg_m[b][:],
                     accum_out=l_parts[:, h, b : b + 1],
                 )
+        copy_values(1, nc.scalar.copy)
 
-        v_grp0 = turn_values(0, "qk2", nc.scalar.copy)
         w_grp = [keep.tile([P, P * 4], BF16, name=f"w_grp{b}", align_bytes=64) for b in range(2)]
         for b in range(2):
             bank = psum.tile([P, 4, P], F32, name="p_t", tag=f"qk{b}")
@@ -210,22 +213,27 @@ def tile_attend_x_ks_bias_srt_kernel(tc, qT, kT, vT, ks, vs, kb, offs, out):
                 in1=vs_col[:].unsqueeze(1).to_broadcast([P, P, 4]),
                 op=ALU.mult,
             )
-        quantize(v_codes, v_scale, block(0), v_grp0[:])
         l_sum = keep.tile([P, 2], F32, name="l_sum")
-        inv_l = keep.tile([P, 2], F32, name="inv_l")
         nc.vector.tensor_tensor(out=l_sum[:], in0=l_parts[:, 0, :], in1=l_parts[:, 1, :], op=ALU.add)
+
+        w_codes = [
+            shared.tile([P, P], U32, name="w_codes0", offset=P_LAST_AT, align_bytes=64),
+            keep.tile([P, P], U32, name="w_codes1", align_bytes=64),
+        ]
+        w_scale = [keep.tile([P, P], U8, name=f"w_scale{b}", align_bytes=64) for b in range(2)]
+        inv_l = shared.tile([P, 2], F32, name="inv_l", offset=P_LAST_AT + 1024, align_bytes=64)
+        quantize(w_codes[0], w_scale[0], block(0), w_grp[0][:])
+        quantize(v_codes[1], v_scale[1], block(0), v_grp[1][:])
+        quantize(w_codes[1], w_scale[1], block(0), w_grp[1][:])
         nc.vector.reciprocal(inv_l[:], l_sum[:])
 
         for b in range(2):
-            w_codes = keep.tile([P, P], U32, name=f"w_codes{b}", align_bytes=64)
-            w_scale = keep.tile([P, P], U8, name=f"w_scale{b}", align_bytes=64)
-            quantize(w_codes, w_scale, block(0), w_grp[b][:])
             y = keep.tile([P, DV], F32, name=f"y{b}")
-            acc = psum.tile([P, P], F32, name="acc_low", tag=f"acc{b}")
-            product(acc[:], w_codes, w_scale, block(0), v_codes, v_scale, block(0))
+            acc = psum.tile([P, P], F32, name="acc_low", tag=("qk2", "qk4")[b])
+            product(acc[:], w_codes[b], w_scale[b], block(0), v_codes[0], v_scale[0], block(0))
             nc.scalar.activation(out=y[:, block(0)], in_=acc[:], func=ACT.Copy, scale=inv_l[:, b : b + 1])
             acc = psum.tile([P, P], F32, name="acc_high", tag=f"s{b}")
-            product(acc[:], w_codes, w_scale, block(0), v_codes, v_scale, block(1))
+            product(acc[:], w_codes[b], w_scale[b], block(0), v_codes[1], v_scale[1], block(0))
             nc.vector.tensor_scalar(
                 out=y[:, block(1)], in0=acc[:], scalar1=inv_l[:, b : b + 1], scalar2=None, op0=ALU.mult
             )

from contextlib import ExitStack

import concourse.mybir as mybir
from concourse.masks import make_identity

P = 128
LAST = P - 1
D, T, N, NQ, DV = 512, 1024, 512, 256, 256
HALF = N // 2
PREFIX = T - HALF
F32 = mybir.dt.float32
BF16 = mybir.dt.bfloat16
U32 = mybir.dt.uint32
U16 = mybir.dt.uint16
U8 = mybir.dt.uint8
FP8X4 = mybir.dt.float8_e4m3fn_x4
ACT = mybir.ActivationFunctionType
ALU = mybir.AluOpType
AX = mybir.AxisListType

V_G_AT = 0
P_LAST_AT = 4096
NEG_M_AT = 6144

FLOPS = 2 * NQ * N * (D + DV)
BYTES = 4 * (D * NQ + (D + DV) * N + 3 * N + NQ * DV) + 2 * N


def tile_attend_x_ks_bias_srt_kernel(tc, qT, kT, vT, ks, vs, kb, offs, out):
    nc = tc.nc
    with ExitStack() as ctx:
        keep = ctx.enter_context(tc.tile_pool(name="keep", bufs=1))
        shared = ctx.enter_context(tc.tile_pool(name="shared", bufs=1))
        psum = ctx.enter_context(tc.psum_pool(name="psum", bufs=1))

        def block(i, width=P):
            return slice(i * width, (i + 1) * width)

        def scalar_cast(dst, src):
            nc.scalar.activation(out=dst, in_=src, func=ACT.Copy)

        def quantize(codes, scales, cols, grouped):
            nc.vector.quantize_mx(out=codes[:, cols].bitcast(FP8X4), scales=scales[:, cols], in_=grouped)

        def product(acc, lhs_codes, lhs_scales, lhs_cols, rhs_codes, rhs_scales, rhs_cols):
            nc.tensor.matmul_mx(
                out=acc,
                lhsT=lhs_codes[:, lhs_cols].bitcast(FP8X4),
                lhsT_scale=lhs_scales[:, lhs_cols],
                rhs=rhs_codes[:, rhs_cols].bitcast(FP8X4),
                rhs_scale=rhs_scales[:, rhs_cols],
                start=True,
                stop=True,
            )

        offsets = keep.tile([P, N // 16], U16, name="offsets")
        ks_row = keep.tile([P, T], F32, name="ks_row")
        kb_row = keep.tile([P, T], F32, name="kb_row")
        vs_row = keep.tile([P, T], F32, name="vs_row")
        ident = keep.tile([P, P], F32, name="ident")
        nc.sync.dma_start(offsets[:], offs)
        for row, table in ((ks_row, ks), (kb_row, kb), (vs_row, vs)):
            nc.scalar.dma_start(row[LAST:, :], table[LAST:, :])
        for row in (ks_row, kb_row):
            nc.vector.memset(row[:LAST, :], 0.0)
        nc.gpsimd.memset(vs_row[:LAST, :], 0.0)
        make_identity(nc, ident[:])

        k_planes = kT.rearrange("(p j) n -> p j n", j=4)
        k_raw = [keep.tile([P, T], F32, name=f"k_raw{j}") for j in range(4)]
        for j in range(3):
            nc.sync.dma_start(k_raw[j][:], k_planes[:, j, :])
        for tokens in (slice(0, PREFIX), slice(PREFIX, T)):
            nc.sync.dma_start(k_raw[3][:, tokens], k_planes[:, 3, tokens])
        q_raw = shared.tile([P, 4, NQ], F32, name="q_raw", offset=0, align_bytes=64)
        nc.sync.dma_start(q_raw[:], qT[0].rearrange("(p j) n -> p j n", j=4))
        v_raw = [keep.tile([P, T], F32, name=f"v_raw{e}") for e in range(2)]
        for e in range(2):
            nc.sync.dma_start(v_raw[e][:], vT[block(e), :])

        def turn_table(row, name, tag, slots, gather):
            gathered = keep.tile([P, N], F32, name=name + "_g")
            gather(gathered[:], row[:].indirect(offsets[:]))
            bank = psum.tile([P, 4, P], F32, name=name + "_t", tag=tag)
            for c in range(4):
                nc.tensor.transpose(bank[:, c, :], gathered[:, slots(c)], ident[:])
            return bank

        ks_bank = turn_table(ks_row, "ks", "s0", block, nc.vector.tensor_copy)
        kb_bank = turn_table(kb_row, "kb", "s1", block, scalar_cast)
        vs_bank = turn_table(vs_row, "vs", "acc0", lambda t: slice(t, N, 4), scalar_cast)

        k_cols = keep.tile([P, 2, 4], F32, name="k_cols")
        scalar_cast(k_cols[:, 0, :4], ks_bank[:, :, LAST])
        scalar_cast(k_cols[:, 1, :4], kb_bank[:, :, LAST])
        vs_col = keep.tile([P, 4], F32, name="vs_col")
        scalar_cast(vs_col[:], vs_bank[:, :, LAST])

        k_g = keep.tile([P, 4, 4, P], BF16, name="k_g", align_bytes=64)
        k_grp = keep.tile([P, N * 4], BF16, name="k_grp", align_bytes=64)
        q_grp = [keep.tile([P, 4 * P], BF16, name=f"q_grp{b}", tag=f"q_grp{b}", align_bytes=64)[:] for b in range(2)]
        q_codes = keep.tile([P, NQ], U32, name="q_codes", align_bytes=64)
        q_scale = keep.tile([P, NQ], U8, name="q_scale", align_bytes=64)
        k_codes = keep.tile([P, N], U32, name="k_codes", align_bytes=64)
        k_scale = keep.tile([P, N], U8, name="k_scale", align_bytes=64)
        for j in range(3):
            nc.vector.tensor_copy(k_g[:, :, j, :], k_raw[j][:].indirect(offsets[:]))
        nc.vector.tensor_copy(k_g[:, :2, 3, :], k_raw[3][:, :PREFIX].indirect(offsets[:, : HALF // 16]))
        for c in (3, 2):
            scalar_cast(k_g[:, c, 3, :], k_raw[3][:].indirect(offsets[:, block(c, P // 16)]))

        def weave(c, engine_copy):
            engine_copy(
                k_grp[:, block(c, 4 * P)].rearrange("p (g i j) -> p g j i", i=4, j=4),
                k_g[:, c, :, :].rearrange("p j (g i) -> p g j i", i=4),
            )

        weave(3, nc.scalar.copy)
        for b in range(2):
            scalar_cast(
                q_grp[b].rearrange("p (c i j) -> p c j i", i=4, j=4),
                q_raw[:, :, block(b)].rearrange("p j (c i) -> p c j i", i=4),
            )
        for c in range(3):
            weave(c, nc.vector.tensor_copy)
        for h in range(2):
            quantize(k_codes, k_scale, block(h, HALF), k_grp[:, block(h, 4 * HALF)])
        for b in range(2):
            quantize(q_codes, q_scale, block(b), q_grp[b])

        s_t = keep.tile([P, 4, NQ], F32, name="s_t", align_bytes=64)
        for b, tag, chunks in (
            (0, "qk0", (0,)),
            (0, "qk1", (1,)),
            (0, "qk2", (2, 3)),
            (1, "qk3", (0, 1)),
            (1, "qk4", (2, 3)),
        ):
            bank = psum.tile([P, len(chunks), P], F32, name="qk", tag=tag)
            for i, c in enumerate(chunks):
                product(bank[:, i, :], k_codes, k_scale, block(c), q_codes, q_scale, block(b))
            for i, c in enumerate(chunks):
                nc.scalar.activation(
                    out=s_t[:, c, block(b)],
                    in_=bank[:, i, :],
                    func=ACT.Identity,
                    scale=k_cols[:, 0, c : c + 1],
                    bias=k_cols[:, 1, c : c + 1],
                )

        v_early = shared.tile([P, N], BF16, name="v_early", offset=V_G_AT, align_bytes=64)
        v_late = keep.tile([P, N], BF16, name="v_late", tag="q_grp1", align_bytes=64)
        v_g = [v_early[:], v_late[:]]
        for e in range(2):
            nc.vector.tensor_copy(v_g[e].rearrange("p (u s h) -> p s u h", u=2, h=2), v_raw[e][:].indirect(offsets[:]))

        s_banks = [psum.tile([P, N], F32, name=f"s_b{b}", tag=f"s{b}") for b in range(2)]
        for b in range(2):
            for c in range(4):
                nc.tensor.transpose(s_banks[b][:, block(c)], s_t[:, c, block(b)], ident[:])

        neg_m = [keep.tile([P, 1], F32, name="neg_m0"), shared.tile([P, 1], F32, name="neg_m1", offset=NEG_M_AT)]
        for b in range(2):
            nc.vector.tensor_reduce(out=neg_m[b][:], in_=s_banks[b][:], axis=AX.X, op=ALU.max, negate=True)

        v_banks = [psum.tile([P, 2, P], F32, name=f"v_t{e}", tag=f"qk{4 - e}") for e in range(2)]
        for e in range(2):
            for u in range(2):
                nc.tensor.transpose(v_banks[e][:, u, :], v_g[e].bitcast(F32)[:, block(u)], ident[:])
        v_grp = [
            keep.tile([P, P * 4], BF16, name="v_grp0", align_bytes=64),
            shared.tile([P, P * 4], BF16, name="v_grp1", offset=NEG_M_AT, align_bytes=64),
        ]
        v_codes = [
            keep.tile([P, P], U32, name="v_codes0", align_bytes=64),
            shared.tile([P, P], U32, name="v_codes1", offset=P_LAST_AT + 512, align_bytes=64),
        ]
        v_scale = [keep.tile([P, P], U8, name=f"v_scale{e}", align_bytes=64) for e in range(2)]

        def copy_values(e, engine_copy):
            engine_copy(
                v_grp[e][:].bitcast(F32).rearrange("p (r u) -> p r u", u=2), v_banks[e][:].rearrange("p u r -> p r u")
            )

        copy_values(0, nc.vector.tensor_copy)
        quantize(v_codes[0], v_scale[0], block(0), v_grp[0][:])

        p_tiles = [
            keep.tile([P, 4, P], F32, name="p0"),
            shared.tile([P, 4, P], F32, name="p1", offset=P_LAST_AT, align_bytes=64),
        ]
        l_parts = keep.tile([P, 2, 2], F32, name="l_parts")
        for b in range(2):
            dealt = s_banks[b][:].rearrange("p (s t) -> p t s", t=4)
            for h in range(2):
                nc.scalar.activation(
                    out=p_tiles[b][:, block(h, 2), :],
                    in_=dealt[:, block(h, 2), :],
                    func=ACT.Exp,
                    bias=neg_m[b][:],
                    accum_out=l_parts[:, h, b : b + 1],
                )
        copy_values(1, nc.scalar.copy)

        w_grp = [keep.tile([P, P * 4], BF16, name=f"w_grp{b}", align_bytes=64) for b in range(2)]
        for b in range(2):
            bank = psum.tile([P, 4, P], F32, name="p_t", tag=f"qk{b}")
            for t in range(4):
                nc.tensor.transpose(bank[:, t, :], p_tiles[b][:, t, :], ident[:])
            nc.vector.tensor_tensor(
                out=w_grp[b][:].rearrange("p (q t) -> p q t", t=4),
                in0=bank[:].rearrange("p t q -> p q t"),
                in1=vs_col[:].unsqueeze(1).to_broadcast([P, P, 4]),
                op=ALU.mult,
            )
        l_sum = keep.tile([P, 2], F32, name="l_sum")
        nc.vector.tensor_tensor(out=l_sum[:], in0=l_parts[:, 0, :], in1=l_parts[:, 1, :], op=ALU.add)

        w_codes = [
            shared.tile([P, P], U32, name="w_codes0", offset=P_LAST_AT, align_bytes=64),
            keep.tile([P, P], U32, name="w_codes1", align_bytes=64),
        ]
        w_scale = [keep.tile([P, P], U8, name=f"w_scale{b}", align_bytes=64) for b in range(2)]
        inv_l = shared.tile([P, 2], F32, name="inv_l", offset=P_LAST_AT + 1024, align_bytes=64)
        quantize(w_codes[0], w_scale[0], block(0), w_grp[0][:])
        quantize(v_codes[1], v_scale[1], block(0), v_grp[1][:])
        quantize(w_codes[1], w_scale[1], block(0), w_grp[1][:])
        nc.vector.reciprocal(inv_l[:], l_sum[:])

        for b in range(2):
            y = keep.tile([P, DV], F32, name=f"y{b}")
            acc = psum.tile([P, P], F32, name="acc_low", tag=("qk2", "qk4")[b])
            product(acc[:], w_codes[b], w_scale[b], block(0), v_codes[0], v_scale[0], block(0))
            nc.scalar.activation(out=y[:, block(0)], in_=acc[:], func=ACT.Copy, scale=inv_l[:, b : b + 1])
            acc = psum.tile([P, P], F32, name="acc_high", tag=f"s{b}")
            product(acc[:], w_codes[b], w_scale[b], block(0), v_codes[1], v_scale[1], block(0))
            nc.vector.tensor_scalar(
                out=y[:, block(1)], in0=acc[:], scalar1=inv_l[:, b : b + 1], scalar2=None, op0=ALU.mult
            )
            nc.sync.dma_start(out[0, block(b), :], y[:])
